import numpy as np
import ml_dtypes


def mxq(x, axis, fmt="e4m3"):
    dtype, down = {"e4m3": (ml_dtypes.float8_e4m3fn, 7), "e5m2": (ml_dtypes.float8_e5m2, 14)}[fmt]
    v = np.moveaxis(np.asarray(x, np.float32).astype(ml_dtypes.bfloat16).astype(np.float64), axis, -1)
    blocks = v.reshape(v.shape[:-1] + (-1, 32))
    amax = np.abs(blocks).max(-1, keepdims=True)
    byte = np.maximum(np.where(amax > 0, np.frexp(amax)[1] - 1 + 127, 0) - down, 1)
    scale = np.exp2(byte - 127.0)
    codes = (blocks / scale).astype(np.float32).astype(dtype).astype(np.float64)
    return np.moveaxis((codes * scale).reshape(v.shape), -1, axis)


WIDE = False


def mx_kscale(k):
    if not WIDE:
        return np.ones(k)
    levels = np.array([10, -10, 5, -5, 0])
    if k % 512:
        return np.exp2(np.random.permutation(np.resize(levels, k // 32))).repeat(32)
    a = np.empty((k // 512, 16))
    for p in range(k // 512):
        a[p, :8] = np.random.permutation(np.resize(levels, 8))
        for g in range(8):
            far = levels[np.abs(levels - a[p, g]) >= 10]
            a[p, g + 8] = far[np.random.randint(len(far))]
    return np.exp2(a.ravel()).repeat(32)


def f64(x):
    return np.asarray(x).astype(np.float64)


def striped(idx):
    return np.tile(idx.reshape(-1, 16).T, (8, 1)).astype(np.uint16)


def unstriped(offs):
    return offs[:16].T.reshape(-1).astype(np.int64)


E2M1 = np.array([0.0, 0.5, 1.0, 1.5, 2.0, 3.0, 4.0, 6.0, -0.0, -0.5, -1.0, -1.5, -2.0, -3.0, -4.0, -6.0])


def pack_weight(w, fmt):
    k, n = w.shape
    w = f64(np.asarray(w, np.float32).astype(ml_dtypes.bfloat16)).reshape(k // 32, 32, n)
    amax = np.abs(w).max(1)
    if fmt == "e4m3":
        byte = np.frexp(amax)[1] - 1 + 127 - 7
    else:
        mant, ex = np.frexp(amax / 6.0)
        byte = np.where(mant > 0.5, ex, ex - 1) + 127
    byte = np.clip(np.where(amax > 0, byte, 1), 1, 254)
    scaled = (w * np.exp2(127.0 - byte)[:, None, :]).reshape(k, n).astype(np.float32)
    by_word = np.ascontiguousarray(scaled.reshape(k // 512, 128, 4, n).transpose(0, 1, 3, 2))
    if fmt == "e4m3":
        words = by_word.astype(ml_dtypes.float8_e4m3fn).view(np.uint8)
    else:
        c = by_word.astype(ml_dtypes.float4_e2m1fn).view(np.uint8) & 0xF
        words = (c[..., 0::2] | (c[..., 1::2] << 4)).reshape(k // 512, 128, 2 * n)
    return np.ascontiguousarray(words), np.ascontiguousarray(byte.astype(np.uint8).reshape(k // 512, 16, n))


def unpack_weight(words, scales, fmt):
    g, _, n = scales.shape
    words = np.ascontiguousarray(words).reshape(g, 128, n, -1)
    if fmt == "e4m3":
        vals = words.view(ml_dtypes.float8_e4m3fn).astype(np.float64)
    else:
        nib = np.empty((g, 128, n, 4), np.uint8)
        nib[..., 0::2] = words & 0xF
        nib[..., 1::2] = words >> 4
        vals = E2M1[nib]
    vals = vals * np.repeat(np.exp2(scales.astype(np.float64) - 127.0), 8, axis=1)[..., None]
    return vals.transpose(0, 1, 3, 2).reshape(g * 512, n)


def relu(v):
    return np.maximum(v, 0.0)


K, T, E, C, N = 1024, 1024, 8, 256, 128
K8 = 512


def by_expert(wq, xq):
    return np.concatenate([wq[e].T @ xq[:, e * C:(e + 1) * C] for e in range(E)], axis=1)


def setup_inputs():
    n = np.random.standard_normal
    s = mx_kscale(K)[:, None]
    first = np.random.permutation(np.repeat(np.arange(E), T // E))
    second = (first + 1 + np.random.permutation(np.repeat(np.arange(E - 1), -(-T // (E - 1)))[:T])) % E
    while np.bincount(second, minlength=E).max() != T // E:
        load = np.bincount(second, minlength=E); hi, lo = int(load.argmax()), int(load.argmin())
        t = np.flatnonzero((second == hi) & (first != lo))[0]; second[t] = lo
    slot_token = np.empty(E * C, np.int64); pos = np.empty((2, T), np.int64); fill = np.zeros(E, np.int64)
    place = np.stack([np.random.permutation(C) for _ in range(E)])
    for r, deal in enumerate((first, second)):
        for t in np.random.permutation(T):
            e = deal[t]; j = e * C + place[e, fill[e]]; fill[e] += 1; slot_token[j] = t; pos[r, t] = j
    g = np.random.uniform(0.2, 0.8, T)
    w = n((E, K, N)) / np.sqrt(K) / s[None]
    w8 = [pack_weight(m[:K8], "e4m3") for m in w]
    w4 = [pack_weight(m[K8:], "e2m1") for m in w]
    return {
        "xT": (n((K, T)) * s).astype(np.float32),
        "w8_words": np.stack([m[0] for m in w8]),
        "w8_scales": np.stack([m[1] for m in w8]),
        "w4_words": np.stack([m[0] for m in w4]),
        "w4_scales": np.stack([m[1] for m in w4]),
        "b": (0.3 * n((N, E))).astype(np.float32),
        "gate": np.stack([np.tile(g, (N, 1)), np.tile(1.0 - g, (N, 1))]).astype(np.float32),
        "offs": striped(slot_token),
        "pos1": striped(pos[0]),
        "pos2": striped(pos[1]),
    }


def reference(xT, w8_words, w8_scales, w4_words, w4_scales, b, gate, offs, pos1, pos2):
    idx = unstriped(offs)
    w = np.stack([np.concatenate([unpack_weight(w8_words[e], w8_scales[e], "e4m3"), unpack_weight(w4_words[e], w4_scales[e], "e2m1")]) for e in range(E)])
    xq = mxq(f64(xT)[:, idx], 0, "e4m3")
    y = by_expert(w, xq)
    y = relu(y + np.repeat(f64(b), C, axis=1))
    return f64(gate[0]) * y[:, unstriped(pos1)] + f64(gate[1]) * y[:, unstriped(pos2)]

@@ -1,0 +1,184 @@
+from contextlib import ExitStack
+
+import concourse.mybir as mybir
+
+K, T, E, C, N = 1024, 1024, 8, 256, 128
+SLOTS = E * C
+FLOPS = 2 * SLOTS * K * N
+
+F32 = mybir.dt.float32
+BF16 = mybir.dt.bfloat16
+I32 = mybir.dt.int32
+U32 = mybir.dt.uint32
+U16 = mybir.dt.uint16
+U8 = mybir.dt.uint8
+FP8X4 = mybir.dt.float8_e4m3fn_x4
+FP4X4 = mybir.dt.float4_e2m1fn_x4
+COPY = mybir.ActivationFunctionType.Copy
+RELU = mybir.ActivationFunctionType.Relu
+MULT = mybir.AluOpType.mult
+ADD = mybir.AluOpType.add
+MAX = mybir.AluOpType.max
+
+P = 128
+PASSES = 2
+FIRST_ROW = (4, 0)
+LOADS = (
+    ((0, 512), (512, 768), (768, 896), (896, 1024)),
+    ((0, 256), (256, 512), (512, 768), (768, 896), (896, 1024)),
+)
+VECTOR_SHARE = 0.6875
+HALF = 128
+
+
+def tile_moe_pln_lin_relu_kernel(
+    tc, xT, w8_words, w8_scales, w4_words, w4_scales, b, gate, offs, pos1, pos2, out
+):
+    nc = tc.nc
+    with ExitStack() as ctx:
+        keep = ctx.enter_context(tc.tile_pool(name="keep", bufs=1))
+        psum = ctx.enter_context(tc.psum_pool(name="psum", bufs=1))
+
+        offs_sb = keep.tile([P, SLOTS // 16], U16, name="offs_sb")
+        pos1_sb = keep.tile([P, T // 16], U16, name="pos1_sb")
+        pos2_sb = keep.tile([P, T // 16], U16, name="pos2_sb")
+        w8_sb = keep.tile([P, E, 4 * N], U8, name="w8_sb", align_bytes=64)
+        w4_sb = keep.tile([P, E, 2 * N], U8, name="w4_sb", align_bytes=64)
+        w_scales = keep.tile([P, E * N], U8, name="w_scales", align_bytes=64)
+        x_scales = keep.tile([P, T], U8, name="x_scales", align_bytes=64)
+        slot_scales = keep.tile([P, SLOTS], U8, name="slot_scales", align_bytes=64)
+        x_codes = [keep.tile([P, T], U32, name=f"x_codes{a}", align_bytes=64) for a in range(PASSES)]
+        slot_codes = [keep.tile([P, SLOTS], U32, name=f"slot_codes{a}", align_bytes=64) for a in range(PASSES)]
+        bias = keep.tile([P, E], F32, name="bias")
+        gates = keep.tile([P, 2, T], F32, name="gates")
+        y = keep.tile([P, SLOTS], F32, name="y")
+        warm = keep.tile([P, 8], F32, name="warm")
+
+        nc.gpsimd.memset(warm[:], 0.0)
+        nc.scalar.activation(warm[:, 0:1], warm[:, 1:2], RELU)
+        nc.gpsimd.memset(x_scales[:], 0)
+        nc.gpsimd.memset(w_scales[:].bitcast(I32), 0)
+
+        raw = {}
+        for a in range(PASSES):
+            for lo, hi in LOADS[a]:
+                raw[a, lo] = keep.tile([P, 4, hi - lo], F32, name=f"raw{a}_{lo}")
+                nc.sync.dma_start(
+                    raw[a, lo][:],
+                    xT[512 * a : 512 * (a + 1), lo:hi].rearrange("(p j) t -> p j t", j=4),
+                )
+            if a == 0:
+                nc.sync.dma_start(offs_sb[:], offs)
+        nc.sync.dma_start(w8_sb[:].bitcast(I32), w8_words[:, 0].rearrange("e p n r -> p e (n r)").bitcast(I32))
+        nc.sync.dma_start(w4_sb[:].bitcast(I32), w4_words[:, 0].rearrange("e p m -> p e m").bitcast(I32))
+        for source, first in ((w8_scales, FIRST_ROW[0]), (w4_scales, FIRST_ROW[1])):
+            for q in range(4):
+                nc.sync.dma_start(
+                    w_scales[32 * q + first : 32 * q + first + 4, :].bitcast(I32).rearrange("q (e n) -> q e n", e=E),
+                    source[:, 0, 4 * q : 4 * q + 4, :].rearrange("e q n -> q e n").bitcast(I32),
+                )
+        nc.sync.dma_start(bias[:], b)
+        nc.sync.dma_start(pos1_sb[:], pos1)
+        nc.sync.dma_start(pos2_sb[:], pos2)
+        nc.sync.dma_start(gates[:], gate.rearrange("g n t -> n g t"))
+
+        grouped = [keep.tile([P, T, 4], BF16, name=f"grouped{a}", align_bytes=64) for a in range(PASSES)]
+
+        def interleave(copy, a, lo, hi, first):
+            copy(
+                grouped[a][:, lo:hi, :].rearrange("p (c i) j -> p c j i", i=4),
+                raw[a, first][:, :, lo - first : hi - first].rearrange("p j (c i) -> p c j i", i=4),
+            )
+
+        def scalar_copy(dst, src):
+            nc.scalar.activation(dst, src, COPY)
+
+        def cast(a, lo, hi, vector_share):
+            v = lo + int((hi - lo) * vector_share)
+            if v > lo:
+                interleave(nc.vector.tensor_copy, a, lo, v, lo)
+            if v < hi:
+                interleave(scalar_copy, a, v, hi, lo)
+
+        def quantize(a, lo, hi):
+            nc.vector.quantize_mx(
+                out=x_codes[a][:, lo:hi].bitcast(FP8X4),
+                scales=x_scales[FIRST_ROW[a] : P, lo:hi],
+                in_=grouped[a][:, lo:hi, :].rearrange("p t j -> p (t j)"),
+            )
+
+        def gather_codes(a, lo, hi):
+            nc.vector.tensor_copy(slot_codes[a][:, lo:hi], x_codes[a][:].indirect(offs_sb[:, lo // 16 : hi // 16]))
+
+        def gather_scales(lo, hi):
+            nc.vector.tensor_copy(slot_scales[:, lo:hi], x_scales[:].indirect(offs_sb[:, lo // 16 : hi // 16]))
+
+        banks = []
+
+        def multiply(lo, hi):
+            e = lo // C
+            acc = psum.tile([P, C], F32, name=f"acc{len(banks) % 8}")
+            banks.append(acc)
+            for s in range(lo, hi, HALF):
+                cols = slice(s - lo, s - lo + HALF)
+                for a in range(PASSES):
+                    weights = w8_sb[:, e, :].bitcast(FP8X4) if a == 0 else w4_sb[:, e, :].bitcast(FP4X4)
+                    nc.tensor.matmul_mx(
+                        out=acc[:, cols],
+                        lhsT=weights,
+                        lhsT_scale=w_scales[FIRST_ROW[a] : P, e * N : (e + 1) * N],
+                        rhs=slot_codes[a][:, s : s + HALF].bitcast(FP8X4),
+                        rhs_scale=slot_scales[FIRST_ROW[a] : P, s : s + HALF],
+                        start=(a == 0),
+                        stop=(a == PASSES - 1),
+                    )
+            if hi == SLOTS:
+                nc.vector.tensor_scalar(y[:, lo:hi], acc[:, 0 : hi - lo], bias[:, e : e + 1], 0.0, ADD, MAX)
+            else:
+                nc.scalar.activation(y[:, lo:hi], acc[:, 0 : hi - lo], RELU, bias=bias[:, e : e + 1])
+
+        for lo, hi in LOADS[0]:
+            cast(0, lo, hi, 0.5 if lo == 0 else VECTOR_SHARE)
+            quantize(0, lo, hi)
+        gather_codes(0, 0, 768)
+        gather_codes(0, 768, 1536)
+        for lo, hi in LOADS[1]:
+            cast(1, lo, hi, 0.0)
+        quantize(1, 0, 512)
+        gather_codes(0, 1536, 1920)
+        quantize(1, 512, 768)
+        quantize(1, 768, 896)
+        quantize(1, 896, 1024)
+        gather_codes(0, 1920, 2048)
+        for lo, hi in ((0, 768), (768, 1536)):
+            gather_scales(lo, hi)
+            gather_codes(1, lo, hi)
+            for s in range(lo, hi, C):
+                multiply(s, s + C)
+        gather_scales(1536, 2048)
+        gather_codes(1, 1536, 1920)
+        multiply(1536, 1792)
+        multiply(1792, 1920)
+        gather_codes(1, 1920, 2048)
+        multiply(1920, 2048)
+
+        first = keep.tile([P, T], F32, name="first")
+        second = keep.tile([P, T], F32, name="second")
+        result = keep.tile([P, T], F32, name="result")
+
+        def second_choice(lo, hi):
+            nc.vector.tensor_tensor(
+                second[:, lo:hi], y[:].indirect(pos2_sb[:, lo // 16 : hi // 16]), gates[:, 1, lo:hi], MULT
+            )
+
+        def add_and_store(lo, hi):
+            nc.vector.tensor_add(result[:, lo:hi], first[:, lo:hi], second[:, lo:hi])
+            nc.sync.dma_start(out[:, lo:hi], result[:, lo:hi])
+
+        nc.vector.tensor_tensor(first[:], y[:].indirect(pos1_sb[:]), gates[:, 0, :], MULT)
+        second_choice(0, 512)
+        second_choice(512, 768)
+        add_and_store(0, 512)
+        second_choice(768, 1024)
+        add_and_store(512, 768)
+        add_and_store(768, 1024)

@@ -23,12 +23,10 @@ MAX = mybir.AluOpType.max
 P = 128
 PASSES = 2
 FIRST_ROW = (4, 0)
-LOADS = (
-    ((0, 512), (512, 768), (768, 896), (896, 1024)),
-    ((0, 256), (256, 512), (512, 768), (768, 896), (896, 1024)),
-)
-VECTOR_SHARE = 0.6875
 HALF = 128
+TURNED = 0
+CHUNK = 256
+WINDOW = 4096
 
 
 def tile_moe_pln_lin_relu_kernel(
@@ -47,10 +45,10 @@ def tile_moe_pln_lin_relu_kernel(
         w_scales = keep.tile([P, E * N], U8, name="w_scales", align_bytes=64)
         x_scales = keep.tile([P, T], U8, name="x_scales", align_bytes=64)
         slot_scales = keep.tile([P, SLOTS], U8, name="slot_scales", align_bytes=64)
-        x_codes = [keep.tile([P, T], U32, name=f"x_codes{a}", align_bytes=64) for a in range(PASSES)]
+        x_codes = [keep.tile([P, WINDOW if a == 1 else T], U32, name=f"x_codes{a}", align_bytes=64) for a in range(PASSES)]
         slot_codes = [keep.tile([P, SLOTS], U32, name=f"slot_codes{a}", align_bytes=64) for a in range(PASSES)]
         bias = keep.tile([P, E], F32, name="bias")
-        gates = keep.tile([P, 2, T], F32, name="gates")
+        gates = keep.tile([P, 2, T - TURNED], F32, name="gates")
         y = keep.tile([P, SLOTS], F32, name="y")
         warm = keep.tile([P, 8], F32, name="warm")
 
@@ -58,19 +56,64 @@ def tile_moe_pln_lin_relu_kernel(
         nc.scalar.activation(warm[:, 0:1], warm[:, 1:2], RELU)
         nc.gpsimd.memset(x_scales[:], 0)
         nc.gpsimd.memset(w_scales[:].bitcast(I32), 0)
+        nc.vector.memset(x_codes[1][:, T:WINDOW].bitcast(I32), 0)
 
+        grouped = [keep.tile([P, T, 4], BF16, name=f"grouped{a}", align_bytes=64) for a in range(PASSES)]
         raw = {}
-        for a in range(PASSES):
-            for lo, hi in LOADS[a]:
-                raw[a, lo] = keep.tile([P, 4, hi - lo], F32, name=f"raw{a}_{lo}")
-                nc.sync.dma_start(
-                    raw[a, lo][:],
-                    xT[512 * a : 512 * (a + 1), lo:hi].rearrange("(p j) t -> p j t", j=4),
-                )
-            if a == 0:
-                nc.sync.dma_start(offs_sb[:], offs)
-        nc.sync.dma_start(w8_sb[:].bitcast(I32), w8_words[:, 0].rearrange("e p n r -> p e (n r)").bitcast(I32))
+
+        def load(a, j0, j1, lo, hi):
+            raw[a, j0, lo] = keep.tile([P, j1 - j0, hi - lo], F32, name=f"raw{a}_{j0}_{lo}")
+            nc.sync.dma_start(
+                raw[a, j0, lo][:],
+                xT[512 * a : 512 * (a + 1), lo:hi].rearrange("(p j) t -> p j t", j=4)[:, j0:j1, :],
+            )
+
+        def scalar_copy(dst, src):
+            nc.scalar.activation(dst, src, COPY)
+
+        def interleave(copy, a, j0, j1, first, lo, hi):
+            copy(
+                grouped[a][:, lo:hi, j0:j1].rearrange("p (c i) j -> p c j i", i=4),
+                raw[a, j0, first][:, :, lo - first : hi - first].rearrange("p j (c i) -> p c j i", i=4),
+            )
+
+        def cast(a, j0, j1, lo, hi, vector_tokens):
+            v = lo + vector_tokens
+            if v > lo:
+                interleave(nc.vector.tensor_copy, a, j0, j1, lo, lo, v)
+            if v < hi:
+                interleave(scalar_copy, a, j0, j1, lo, v, hi)
+
+        def quantize(a, lo, hi):
+            nc.vector.quantize_mx(
+                out=x_codes[a][:, lo:hi].bitcast(FP8X4),
+                scales=x_scales[FIRST_ROW[a] : P, lo:hi],
+                in_=grouped[a][:, lo:hi, :].rearrange("p t j -> p (t j)"),
+            )
+
+        def gather_codes(a, lo, hi, window=T):
+            nc.vector.tensor_copy(slot_codes[a][:, lo:hi], x_codes[a][:, 0:window].indirect(offs_sb[:, lo // 16 : hi // 16]))
+
+        def gather_scales(lo, hi):
+            nc.vector.tensor_copy(slot_scales[:, lo:hi], x_scales[:].indirect(offs_sb[:, lo // 16 : hi // 16]))
+
+        load(1, 0, 4, 0, 256)
+        load(1, 0, 4, 256, 512)
+        load(1, 0, 4, 512, 768)
+        load(1, 0, 4, 768, 896)
+        load(1, 0, 4, 896, 960)
+        load(1, 0, 4, 960, 1024)
+        nc.sync.dma_start(offs_sb[:], offs)
+        load(0, 0, 4, 0, 128)
+        load(0, 0, 4, 128, 256)
+        load(0, 0, 4, 256, 384)
+        load(0, 0, 4, 384, 512)
+        load(0, 0, 4, 512, 640)
+        load(0, 0, 4, 640, 768)
+        load(0, 0, 4, 768, 896)
+        load(0, 0, 4, 896, 1024)
         nc.sync.dma_start(w4_sb[:].bitcast(I32), w4_words[:, 0].rearrange("e p m -> p e m").bitcast(I32))
+        nc.sync.dma_start(w8_sb[:].bitcast(I32), w8_words[:, 0].rearrange("e p n r -> p e (n r)").bitcast(I32))
         for source, first in ((w8_scales, FIRST_ROW[0]), (w4_scales, FIRST_ROW[1])):
             for q in range(4):
                 nc.sync.dma_start(
@@ -80,105 +123,100 @@ def tile_moe_pln_lin_relu_kernel(
         nc.sync.dma_start(bias[:], b)
         nc.sync.dma_start(pos1_sb[:], pos1)
         nc.sync.dma_start(pos2_sb[:], pos2)
-        nc.sync.dma_start(gates[:], gate.rearrange("g n t -> n g t"))
-
-        grouped = [keep.tile([P, T, 4], BF16, name=f"grouped{a}", align_bytes=64) for a in range(PASSES)]
-
-        def interleave(copy, a, lo, hi, first):
-            copy(
-                grouped[a][:, lo:hi, :].rearrange("p (c i) j -> p c j i", i=4),
-                raw[a, first][:, :, lo - first : hi - first].rearrange("p j (c i) -> p c j i", i=4),
-            )
-
-        def scalar_copy(dst, src):
-            nc.scalar.activation(dst, src, COPY)
-
-        def cast(a, lo, hi, vector_share):
-            v = lo + int((hi - lo) * vector_share)
-            if v > lo:
-                interleave(nc.vector.tensor_copy, a, lo, v, lo)
-            if v < hi:
-                interleave(scalar_copy, a, v, hi, lo)
-
-        def quantize(a, lo, hi):
-            nc.vector.quantize_mx(
-                out=x_codes[a][:, lo:hi].bitcast(FP8X4),
-                scales=x_scales[FIRST_ROW[a] : P, lo:hi],
-                in_=grouped[a][:, lo:hi, :].rearrange("p t j -> p (t j)"),
-            )
-
-        def gather_codes(a, lo, hi):
-            nc.vector.tensor_copy(slot_codes[a][:, lo:hi], x_codes[a][:].indirect(offs_sb[:, lo // 16 : hi // 16]))
-
-        def gather_scales(lo, hi):
-            nc.vector.tensor_copy(slot_scales[:, lo:hi], x_scales[:].indirect(offs_sb[:, lo // 16 : hi // 16]))
+        nc.sync.dma_start(gates[:], gate[:, :, TURNED:T].rearrange("g n t -> n g t"))
 
         banks = []
 
-        def multiply(lo, hi):
-            e = lo // C
-            acc = psum.tile([P, C], F32, name=f"acc{len(banks) % 8}")
-            banks.append(acc)
-            for s in range(lo, hi, HALF):
-                cols = slice(s - lo, s - lo + HALF)
-                for a in range(PASSES):
-                    weights = w8_sb[:, e, :].bitcast(FP8X4) if a == 0 else w4_sb[:, e, :].bitcast(FP4X4)
-                    nc.tensor.matmul_mx(
-                        out=acc[:, cols],
-                        lhsT=weights,
-                        lhsT_scale=w_scales[FIRST_ROW[a] : P, e * N : (e + 1) * N],
-                        rhs=slot_codes[a][:, s : s + HALF].bitcast(FP8X4),
-                        rhs_scale=slot_scales[FIRST_ROW[a] : P, s : s + HALF],
-                        start=(a == 0),
-                        stop=(a == PASSES - 1),
-                    )
-            if hi == SLOTS:
-                nc.vector.tensor_scalar(y[:, lo:hi], acc[:, 0 : hi - lo], bias[:, e : e + 1], 0.0, ADD, MAX)
-            else:
-                nc.scalar.activation(y[:, lo:hi], acc[:, 0 : hi - lo], RELU, bias=bias[:, e : e + 1])
+        def new_bank():
+            banks.append(psum.tile([P, C], F32, name=f"acc{len(banks) % 8}"))
+            return banks[-1]
 
-        for lo, hi in LOADS[0]:
-            cast(0, lo, hi, 0.5 if lo == 0 else VECTOR_SHARE)
-            quantize(0, lo, hi)
-        gather_codes(0, 0, 768)
-        gather_codes(0, 768, 1536)
-        for lo, hi in LOADS[1]:
-            cast(1, lo, hi, 0.0)
-        quantize(1, 0, 512)
-        gather_codes(0, 1536, 1920)
+        def one_pass(a, acc, s):
+            e = s // C
+            weights = w8_sb[:, e, :].bitcast(FP8X4) if a == 0 else w4_sb[:, e, :].bitcast(FP4X4)
+            nc.tensor.matmul_mx(
+                out=acc,
+                lhsT=weights,
+                lhsT_scale=w_scales[FIRST_ROW[a] : P, e * N : (e + 1) * N],
+                rhs=slot_codes[a][:, s : s + HALF].bitcast(FP8X4),
+                rhs_scale=slot_scales[FIRST_ROW[a] : P, s : s + HALF],
+                start=(a == 1),
+                stop=(a == 0),
+            )
+
+        def relu(acc, lo, hi):
+            e = lo // C
+            if hi == SLOTS:
+                nc.vector.tensor_scalar(y[:, lo:hi], acc, bias[:, e : e + 1], 0.0, ADD, MAX)
+            else:
+                nc.scalar.activation(y[:, lo:hi], acc, RELU, bias=bias[:, e : e + 1])
+
+        def multiply(lo, hi):
+            acc = new_bank()
+            for s in range(lo, hi, HALF):
+                for a in (1, 0):
+                    one_pass(a, acc[:, s - lo : s - lo + HALF], s)
+            relu(acc[:, 0 : hi - lo], lo, hi)
+
+        cast(1, 0, 4, 0, 256, 64)
+        quantize(1, 0, 256)
+        cast(1, 0, 4, 256, 512, 64)
+        quantize(1, 256, 512)
+        cast(1, 0, 4, 512, 768, 112)
         quantize(1, 512, 768)
+        cast(1, 0, 4, 768, 896, 64)
         quantize(1, 768, 896)
-        quantize(1, 896, 1024)
-        gather_codes(0, 1920, 2048)
+        cast(1, 0, 4, 896, 960, 0)
+        quantize(1, 896, 960)
+        cast(1, 0, 4, 960, 1024, 64)
+        quantize(1, 960, 1024)
+        gather_codes(1, 0, 2048, WINDOW)
+        for lo in range(0, T, 128):
+            cast(0, 0, 4, lo, lo + 128, 0)
+        quantize(0, 0, 512)
+        quantize(0, 512, 768)
+        quantize(0, 768, 1024)
         for lo, hi in ((0, 768), (768, 1536)):
             gather_scales(lo, hi)
-            gather_codes(1, lo, hi)
+            gather_codes(0, lo, hi)
             for s in range(lo, hi, C):
                 multiply(s, s + C)
         gather_scales(1536, 2048)
-        gather_codes(1, 1536, 1920)
-        multiply(1536, 1792)
-        multiply(1792, 1920)
-        gather_codes(1, 1920, 2048)
-        multiply(1920, 2048)
+        pair = new_bank()
+        last = {s: new_bank() for s in (1792, 1920)}
+        one_pass(1, pair[:, 0:HALF], 1536)
+        for s in (1792, 1920):
+            one_pass(1, last[s][:, 0:HALF], s)
+        gather_codes(0, 1536, 1792)
+        one_pass(0, pair[:, 0:HALF], 1536)
+        one_pass(1, pair[:, HALF:C], 1664)
+        one_pass(0, pair[:, HALF:C], 1664)
+        relu(pair[:], 1536, 1792)
+        for s in (1792, 1920):
+            gather_codes(0, s, s + HALF)
+            one_pass(0, last[s][:, 0:HALF], s)
+            relu(last[s][:, 0:HALF], s, s + HALF)
 
-        first = keep.tile([P, T], F32, name="first")
-        second = keep.tile([P, T], F32, name="second")
+        picked = [keep.tile([P, T], F32, name=f"picked{g}") for g in range(2)]
         result = keep.tile([P, T], F32, name="result")
+        pos_sb = (pos1_sb, pos2_sb)
 
-        def second_choice(lo, hi):
+        def looked_up(g, lo, hi):
+            return y[:].indirect(pos_sb[g][:, lo // 16 : hi // 16])
+
+        def gated(g, lo, hi):
             nc.vector.tensor_tensor(
-                second[:, lo:hi], y[:].indirect(pos2_sb[:, lo // 16 : hi // 16]), gates[:, 1, lo:hi], MULT
+                picked[g][:, lo:hi], looked_up(g, lo, hi), gates[:, g, lo - TURNED : hi - TURNED], MULT
             )
 
         def add_and_store(lo, hi):
-            nc.vector.tensor_add(result[:, lo:hi], first[:, lo:hi], second[:, lo:hi])
+            nc.vector.tensor_add(result[:, lo:hi], picked[0][:, lo:hi], picked[1][:, lo:hi])
             nc.sync.dma_start(out[:, lo:hi], result[:, lo:hi])
 
-        nc.vector.tensor_tensor(first[:], y[:].indirect(pos1_sb[:]), gates[:, 0, :], MULT)
-        second_choice(0, 512)
-        second_choice(512, 768)
+        gated(0, 0, 1024)
+        gated(1, 0, 512)
+        gated(1, 512, 768)
         add_and_store(0, 512)
-        second_choice(768, 1024)
+        gated(1, 768, 1024)
         add_and_store(512, 768)
         add_and_store(768, 1024)

@@ -45,7 +45,7 @@ def tile_moe_pln_lin_relu_kernel(
         w_scales = keep.tile([P, E * N], U8, name="w_scales", align_bytes=64)
         x_scales = keep.tile([P, T], U8, name="x_scales", align_bytes=64)
         slot_scales = keep.tile([P, SLOTS], U8, name="slot_scales", align_bytes=64)
-        x_codes = [keep.tile([P, WINDOW if a == 1 else T], U32, name=f"x_codes{a}", align_bytes=64) for a in range(PASSES)]
+        x_codes = [keep.tile([P, WINDOW if a == 0 else T], U32, name=f"x_codes{a}", align_bytes=64) for a in range(PASSES)]
         slot_codes = [keep.tile([P, SLOTS], U32, name=f"slot_codes{a}", align_bytes=64) for a in range(PASSES)]
         bias = keep.tile([P, E], F32, name="bias")
         gates = keep.tile([P, 2, T - TURNED], F32, name="gates")
@@ -56,7 +56,7 @@ def tile_moe_pln_lin_relu_kernel(
         nc.scalar.activation(warm[:, 0:1], warm[:, 1:2], RELU)
         nc.gpsimd.memset(x_scales[:], 0)
         nc.gpsimd.memset(w_scales[:].bitcast(I32), 0)
-        nc.vector.memset(x_codes[1][:, T:WINDOW].bitcast(I32), 0)
+        nc.vector.memset(x_codes[0][:, T:WINDOW].bitcast(I32), 0)
 
         grouped = [keep.tile([P, T, 4], BF16, name=f"grouped{a}", align_bytes=64) for a in range(PASSES)]
         raw = {}
@@ -65,6 +65,15 @@ def tile_moe_pln_lin_relu_kernel(
             raw[a, j0, lo] = keep.tile([P, j1 - j0, hi - lo], F32, name=f"raw{a}_{j0}_{lo}")
             nc.sync.dma_start(
                 raw[a, j0, lo][:],
+                xT[512 * a : 512 * (a + 1), lo:hi].rearrange("(p j) t -> p j t", j=4)[:, j0:j1, :],
+            )
+
+        whole = keep.tile([P, 4, T], F32, name="whole")
+
+        def load_rows(a, j0, j1, lo, hi):
+            raw[a, 0, lo] = whole[:, :, lo:hi]
+            nc.sync.dma_start(
+                whole[:, j0:j1, lo:hi],
                 xT[512 * a : 512 * (a + 1), lo:hi].rearrange("(p j) t -> p j t", j=4)[:, j0:j1, :],
             )
 
@@ -97,23 +106,19 @@ def tile_moe_pln_lin_relu_kernel(
         def gather_scales(lo, hi):
             nc.vector.tensor_copy(slot_scales[:, lo:hi], x_scales[:].indirect(offs_sb[:, lo // 16 : hi // 16]))
 
+        load_rows(0, 0, 2, 0, 1024)
+        load_rows(0, 2, 4, 0, 256)
+        load_rows(0, 2, 4, 256, 512)
+        load_rows(0, 2, 4, 512, 768)
+        load_rows(0, 2, 4, 768, 1024)
+        nc.sync.dma_start(offs_sb[:], offs)
         load(1, 0, 4, 0, 256)
         load(1, 0, 4, 256, 512)
         load(1, 0, 4, 512, 768)
         load(1, 0, 4, 768, 896)
-        load(1, 0, 4, 896, 960)
-        load(1, 0, 4, 960, 1024)
-        nc.sync.dma_start(offs_sb[:], offs)
-        load(0, 0, 4, 0, 128)
-        load(0, 0, 4, 128, 256)
-        load(0, 0, 4, 256, 384)
-        load(0, 0, 4, 384, 512)
-        load(0, 0, 4, 512, 640)
-        load(0, 0, 4, 640, 768)
-        load(0, 0, 4, 768, 896)
-        load(0, 0, 4, 896, 1024)
-        nc.sync.dma_start(w4_sb[:].bitcast(I32), w4_words[:, 0].rearrange("e p m -> p e m").bitcast(I32))
+        load(1, 0, 4, 896, 1024)
         nc.sync.dma_start(w8_sb[:].bitcast(I32), w8_words[:, 0].rearrange("e p n r -> p e (n r)").bitcast(I32))
+        nc.sync.dma_start(w4_sb[:].bitcast(I32), w4_words[:, 0].rearrange("e p m -> p e m").bitcast(I32))
         for source, first in ((w8_scales, FIRST_ROW[0]), (w4_scales, FIRST_ROW[1])):
             for q in range(4):
                 nc.sync.dma_start(
@@ -140,8 +145,8 @@ def tile_moe_pln_lin_relu_kernel(
                 lhsT_scale=w_scales[FIRST_ROW[a] : P, e * N : (e + 1) * N],
                 rhs=slot_codes[a][:, s : s + HALF].bitcast(FP8X4),
                 rhs_scale=slot_scales[FIRST_ROW[a] : P, s : s + HALF],
-                start=(a == 1),
-                stop=(a == 0),
+                start=(a == 0),
+                stop=(a == 1),
             )
 
         def relu(acc, lo, hi):
@@ -154,47 +159,44 @@ def tile_moe_pln_lin_relu_kernel(
         def multiply(lo, hi):
             acc = new_bank()
             for s in range(lo, hi, HALF):
-                for a in (1, 0):
+                for a in (0, 1):
                     one_pass(a, acc[:, s - lo : s - lo + HALF], s)
             relu(acc[:, 0 : hi - lo], lo, hi)
 
-        cast(1, 0, 4, 0, 256, 64)
-        quantize(1, 0, 256)
-        cast(1, 0, 4, 256, 512, 64)
-        quantize(1, 256, 512)
-        cast(1, 0, 4, 512, 768, 112)
-        quantize(1, 512, 768)
-        cast(1, 0, 4, 768, 896, 64)
-        quantize(1, 768, 896)
-        cast(1, 0, 4, 896, 960, 0)
-        quantize(1, 896, 960)
-        cast(1, 0, 4, 960, 1024, 64)
-        quantize(1, 960, 1024)
-        gather_codes(1, 0, 2048, WINDOW)
-        for lo in range(0, T, 128):
-            cast(0, 0, 4, lo, lo + 128, 0)
-        quantize(0, 0, 512)
+        cast(0, 0, 4, 0, 256, 120)
+        quantize(0, 0, 256)
+        cast(0, 0, 4, 256, 512, 120)
+        quantize(0, 256, 512)
+        cast(0, 0, 4, 512, 768, 120)
         quantize(0, 512, 768)
+        cast(0, 0, 4, 768, 1024, 176)
         quantize(0, 768, 1024)
+        gather_codes(0, 0, 2048, WINDOW)
+        for lo, hi in ((0, 256), (256, 512), (512, 768), (768, 896), (896, 1024)):
+            cast(1, 0, 4, lo, hi, 0)
+        quantize(1, 0, 512)
+        quantize(1, 512, 768)
+        quantize(1, 768, 896)
+        quantize(1, 896, 1024)
         for lo, hi in ((0, 768), (768, 1536)):
             gather_scales(lo, hi)
-            gather_codes(0, lo, hi)
+            gather_codes(1, lo, hi)
             for s in range(lo, hi, C):
                 multiply(s, s + C)
         gather_scales(1536, 2048)
         pair = new_bank()
         last = {s: new_bank() for s in (1792, 1920)}
-        one_pass(1, pair[:, 0:HALF], 1536)
-        for s in (1792, 1920):
-            one_pass(1, last[s][:, 0:HALF], s)
-        gather_codes(0, 1536, 1792)
         one_pass(0, pair[:, 0:HALF], 1536)
-        one_pass(1, pair[:, HALF:C], 1664)
+        for s in (1792, 1920):
+            one_pass(0, last[s][:, 0:HALF], s)
+        gather_codes(1, 1536, 1792)
+        one_pass(1, pair[:, 0:HALF], 1536)
         one_pass(0, pair[:, HALF:C], 1664)
+        one_pass(1, pair[:, HALF:C], 1664)
         relu(pair[:], 1536, 1792)
         for s in (1792, 1920):
-            gather_codes(0, s, s + HALF)
-            one_pass(0, last[s][:, 0:HALF], s)
+            gather_codes(1, s, s + HALF)
+            one_pass(1, last[s][:, 0:HALF], s)
             relu(last[s][:, 0:HALF], s, s + HALF)
 
         picked = [keep.tile([P, T], F32, name=f"picked{g}") for g in range(2)]

@@ -1,6 +1,7 @@
 from contextlib import ExitStack
 
 import concourse.mybir as mybir
+from concourse.masks import make_identity
 
 K, T, E, C, N = 1024, 1024, 8, 256, 128
 SLOTS = E * C
@@ -52,10 +53,12 @@ def tile_moe_pln_lin_relu_kernel(
         y = keep.tile([P, SLOTS], F32, name="y")
         warm = keep.tile([P, 8], F32, name="warm")
 
+        identity = keep.tile([P, P], F32, name="identity")
         nc.gpsimd.memset(warm[:], 0.0)
         nc.scalar.activation(warm[:, 0:1], warm[:, 1:2], RELU)
-        nc.gpsimd.memset(x_scales[:], 0)
+        nc.gpsimd.memset(x_scales[:].bitcast(I32), 0)
         nc.gpsimd.memset(w_scales[:].bitcast(I32), 0)
+        make_identity(nc, identity[:])
         nc.vector.memset(x_codes[0][:, T:WINDOW].bitcast(I32), 0)
 
         grouped = [keep.tile([P, T, 4], BF16, name=f"grouped{a}", align_bytes=64) for a in range(PASSES)]
@@ -211,14 +214,39 @@ def tile_moe_pln_lin_relu_kernel(
                 picked[g][:, lo:hi], looked_up(g, lo, hi), gates[:, g, lo - TURNED : hi - TURNED], MULT
             )
 
+        turned_sum = keep.tile([P, T], F32, name="turned_sum")
+
+        turned = {}
+
+        def turn(g, lo, hi):
+            for s in range(lo, hi, P):
+                if g == 0:
+                    turned[s] = new_bank()
+                nc.tensor.matmul(
+                    turned[s][:, 0:P], picked[g][:, s : s + P], identity[:], start=(g == 0), stop=(g == 1), is_transpose=True
+                )
+                if g == 1:
+                    nc.scalar.activation(turned_sum[:, s : s + P], turned[s][:, 0:P], COPY)
+
+        def turn_back_and_store(lo, hi):
+            back = new_bank()
+            for s in range(lo, hi, P):
+                nc.tensor.transpose(back[:, s - lo : s - lo + P], turned_sum[:, s : s + P], identity[:])
+            nc.scalar.activation(result[:, lo:hi], back[:, 0 : hi - lo], COPY)
+            nc.scalar.dma_start(out[:, lo:hi], result[:, lo:hi])
+
         def add_and_store(lo, hi):
             nc.vector.tensor_add(result[:, lo:hi], picked[0][:, lo:hi], picked[1][:, lo:hi])
             nc.sync.dma_start(out[:, lo:hi], result[:, lo:hi])
 
-        gated(0, 0, 1024)
-        gated(1, 0, 512)
+        gated(0, 0, 512)
+        turn(0, 0, 512)
+        for lo in (0, 256):
+            gated(1, lo, lo + 256)
+            turn(1, lo, lo + 256)
+            turn_back_and_store(lo, lo + 256)
+        gated(0, 512, 1024)
         gated(1, 512, 768)
-        add_and_store(0, 512)
         gated(1, 768, 1024)
         add_and_store(512, 768)
         add_and_store(768, 1024)

@@ -44,7 +44,7 @@ def tile_moe_pln_lin_relu_kernel(
         w8_sb = keep.tile([P, E, 4 * N], U8, name="w8_sb", align_bytes=64)
         w4_sb = keep.tile([P, E, 2 * N], U8, name="w4_sb", align_bytes=64)
         w_scales = keep.tile([P, E * N], U8, name="w_scales", align_bytes=64)
-        x_scales = keep.tile([P, T], U8, name="x_scales", align_bytes=64)
+        x_scales = keep.tile([P, 2 * T], U8, name="x_scales", align_bytes=64)
         slot_scales = keep.tile([P, SLOTS], U8, name="slot_scales", align_bytes=64)
         x_codes = [keep.tile([P, WINDOW if a == 0 else T], U32, name=f"x_codes{a}", align_bytes=64) for a in range(PASSES)]
         slot_codes = [keep.tile([P, SLOTS], U32, name=f"slot_codes{a}", align_bytes=64) for a in range(PASSES)]
@@ -85,8 +85,8 @@ def tile_moe_pln_lin_relu_kernel(
 
         def interleave(copy, a, j0, j1, first, lo, hi):
             copy(
-                grouped[a][:, lo:hi, j0:j1].rearrange("p (c i) j -> p c j i", i=4),
-                raw[a, j0, first][:, :, lo - first : hi - first].rearrange("p j (c i) -> p c j i", i=4),
+                grouped[a][:, lo:hi, j0:j1].rearrange("p (c i) j -> p c j i", i=2),
+                raw[a, j0, first][:, :, lo - first : hi - first].rearrange("p j (c i) -> p c j i", i=2),
             )
 
         def cast(a, j0, j1, lo, hi, vector_tokens):
@@ -136,7 +136,7 @@ def tile_moe_pln_lin_relu_kernel(
         banks = []
 
         def new_bank():
-            banks.append(psum.tile([P, C], F32, name=f"acc{len(banks) % 8}"))
+            banks.append(psum.tile([P, 2 * C], F32, name=f"acc{len(banks) % 8}"))
             return banks[-1]
 
         def one_pass(a, acc, s):
@@ -154,7 +154,7 @@ def tile_moe_pln_lin_relu_kernel(
 
         def relu(acc, lo, hi):
             e = lo // C
-            if hi == SLOTS:
+            if hi == SLOTS - HALF:
                 nc.vector.tensor_scalar(y[:, lo:hi], acc, bias[:, e : e + 1], 0.0, ADD, MAX)
             else:
                 nc.scalar.activation(y[:, lo:hi], acc, RELU, bias=bias[:, e : e + 1])
@@ -181,8 +181,8 @@ def tile_moe_pln_lin_relu_kernel(
         quantize(1, 512, 768)
         quantize(1, 768, 896)
         quantize(1, 896, 1024)
+        gather_scales(0, 1536)
         for lo, hi in ((0, 768), (768, 1536)):
-            gather_scales(lo, hi)
             gather_codes(1, lo, hi)
             for s in range(lo, hi, C):
                 multiply(s, s + C)
@@ -196,7 +196,7 @@ def tile_moe_pln_lin_relu_kernel(
         one_pass(1, pair[:, 0:HALF], 1536)
         one_pass(0, pair[:, HALF:C], 1664)
         one_pass(1, pair[:, HALF:C], 1664)
-        relu(pair[:], 1536, 1792)
+        relu(pair[:, 0:C], 1536, 1792)
         for s in (1792, 1920):
             gather_codes(1, s, s + HALF)
             one_pass(1, last[s][:, 0:HALF], s)

@@ -85,8 +85,8 @@ def tile_moe_pln_lin_relu_kernel(
 
         def interleave(copy, a, j0, j1, first, lo, hi):
             copy(
-                grouped[a][:, lo:hi, j0:j1].rearrange("p (c i) j -> p c j i", i=2),
-                raw[a, j0, first][:, :, lo - first : hi - first].rearrange("p j (c i) -> p c j i", i=2),
+                grouped[a][:, lo:hi, j0:j1].rearrange("p (c i) j -> p c j i", i=4),
+                raw[a, j0, first][:, :, lo - first : hi - first].rearrange("p j (c i) -> p c j i", i=4),
             )
 
         def cast(a, j0, j1, lo, hi, vector_tokens):
@@ -166,13 +166,13 @@ def tile_moe_pln_lin_relu_kernel(
                     one_pass(a, acc[:, s - lo : s - lo + HALF], s)
             relu(acc[:, 0 : hi - lo], lo, hi)
 
-        cast(0, 0, 4, 0, 256, 120)
+        cast(0, 0, 4, 0, 256, 200)
         quantize(0, 0, 256)
-        cast(0, 0, 4, 256, 512, 120)
+        cast(0, 0, 4, 256, 512, 128)
         quantize(0, 256, 512)
-        cast(0, 0, 4, 512, 768, 120)
+        cast(0, 0, 4, 512, 768, 128)
         quantize(0, 512, 768)
-        cast(0, 0, 4, 768, 1024, 176)
+        cast(0, 0, 4, 768, 1024, 136)
         quantize(0, 768, 1024)
         gather_codes(0, 0, 2048, WINDOW)
         for lo, hi in ((0, 256), (256, 512), (512, 768), (768, 896), (896, 1024)):

@@ -71,12 +71,12 @@ def tile_moe_pln_lin_relu_kernel(
                 xT[512 * a : 512 * (a + 1), lo:hi].rearrange("(p j) t -> p j t", j=4)[:, j0:j1, :],
             )
 
-        whole = keep.tile([P, 4, T], F32, name="whole")
+        whole = keep.tile([P, 4, T // 2], F32, name="whole")
 
         def load_rows(a, j0, j1, lo, hi):
-            raw[a, 0, lo] = whole[:, :, lo:hi]
+            raw[a, 0, lo] = whole[:, :, lo - T // 2 : hi - T // 2]
             nc.sync.dma_start(
-                whole[:, j0:j1, lo:hi],
+                whole[:, j0:j1, lo - T // 2 : hi - T // 2],
                 xT[512 * a : 512 * (a + 1), lo:hi].rearrange("(p j) t -> p j t", j=4)[:, j0:j1, :],
             )
 
@@ -109,9 +109,8 @@ def tile_moe_pln_lin_relu_kernel(
         def gather_scales(lo, hi):
             nc.vector.tensor_copy(slot_scales[:, lo:hi], x_scales[:].indirect(offs_sb[:, lo // 16 : hi // 16]))
 
-        load_rows(0, 0, 2, 0, 1024)
-        load_rows(0, 2, 4, 0, 256)
-        load_rows(0, 2, 4, 256, 512)
+        load(0, 0, 4, 0, 512)
+        load_rows(0, 0, 2, 512, 1024)
         load_rows(0, 2, 4, 512, 768)
         load_rows(0, 2, 4, 768, 1024)
         nc.sync.dma_start(offs_sb[:], offs)
@@ -166,13 +165,12 @@ def tile_moe_pln_lin_relu_kernel(
                     one_pass(a, acc[:, s - lo : s - lo + HALF], s)
             relu(acc[:, 0 : hi - lo], lo, hi)
 
-        cast(0, 0, 4, 0, 256, 200)
+        cast(0, 0, 4, 0, 512, 256)
         quantize(0, 0, 256)
-        cast(0, 0, 4, 256, 512, 128)
         quantize(0, 256, 512)
-        cast(0, 0, 4, 512, 768, 128)
+        cast(0, 0, 4, 512, 768, 160)
         quantize(0, 512, 768)
-        cast(0, 0, 4, 768, 1024, 136)
+        cast(0, 0, 4, 768, 1024, 160)
         quantize(0, 768, 1024)
         gather_codes(0, 0, 2048, WINDOW)
         for lo, hi in ((0, 256), (256, 512), (512, 768), (768, 896), (896, 1024)):

@@ -47,7 +47,7 @@ def tile_moe_pln_lin_relu_kernel(
         x_scales = keep.tile([P, 2 * T], U8, name="x_scales", align_bytes=64)
         slot_scales = keep.tile([P, SLOTS], U8, name="slot_scales", align_bytes=64)
         x_codes = [keep.tile([P, WINDOW if a == 0 else T], U32, name=f"x_codes{a}", align_bytes=64) for a in range(PASSES)]
-        slot_codes = [keep.tile([P, SLOTS], U32, name=f"slot_codes{a}", align_bytes=64) for a in range(PASSES)]
+        slot_codes = [keep.tile([P, (1920, SLOTS)[a]], U32, name=f"slot_codes{a}", align_bytes=64) for a in range(PASSES)]
         bias = keep.tile([P, E], F32, name="bias")
         gates = keep.tile([P, 2, T - TURNED], F32, name="gates")
         y = keep.tile([P, SLOTS], F32, name="y")
@@ -65,7 +65,7 @@ def tile_moe_pln_lin_relu_kernel(
         raw = {}
 
         def load(a, j0, j1, lo, hi):
-            raw[a, j0, lo] = keep.tile([P, j1 - j0, hi - lo], F32, name=f"raw{a}_{j0}_{lo}")
+            raw[a, j0, lo] = keep.tile([P, j1 - j0, hi - lo], F32, name=f"raw{a}_{j0}_{lo}", align_bytes=64)
             nc.sync.dma_start(
                 raw[a, j0, lo][:],
                 xT[512 * a : 512 * (a + 1), lo:hi].rearrange("(p j) t -> p j t", j=4)[:, j0:j1, :],
@@ -145,7 +145,7 @@ def tile_moe_pln_lin_relu_kernel(
                 out=acc,
                 lhsT=weights,
                 lhsT_scale=w_scales[FIRST_ROW[a] : P, e * N : (e + 1) * N],
-                rhs=slot_codes[a][:, s : s + HALF].bitcast(FP8X4),
+                rhs=(late_codes[:] if (a, s) == (0, 1920) else slot_codes[a][:, s : s + HALF]).bitcast(FP8X4),
                 rhs_scale=slot_scales[FIRST_ROW[a] : P, s : s + HALF],
                 start=(a == 0),
                 stop=(a == 1),
@@ -172,13 +172,15 @@ def tile_moe_pln_lin_relu_kernel(
         quantize(0, 512, 768)
         cast(0, 0, 4, 768, 1024, 160)
         quantize(0, 768, 1024)
-        gather_codes(0, 0, 2048, WINDOW)
+        nc.vector.tensor_copy(slot_codes[0][:, 0:1920], x_codes[0][:].indirect(offs_sb[:, 0 : 1920 // 16]))
         for lo, hi in ((0, 256), (256, 512), (512, 768), (768, 896), (896, 1024)):
             cast(1, 0, 4, lo, hi, 0)
         quantize(1, 0, 512)
         quantize(1, 512, 768)
         quantize(1, 768, 896)
         quantize(1, 896, 1024)
+        late_codes = keep.tile([P, HALF], U32, name="raw1_0_896", align_bytes=64)
+        nc.vector.tensor_copy(late_codes[:], x_codes[0][:, 0:T].indirect(offs_sb[:, 1920 // 16 : SLOTS // 16]))
         gather_scales(0, 1536)
         for lo, hi in ((0, 768), (768, 1536)):
             gather_codes(1, lo, hi)

@@ -28,6 +28,7 @@ HALF = 128
 TURNED = 0
 CHUNK = 256
 WINDOW = 4096
+EARLY = 1920
 
 
 def tile_moe_pln_lin_relu_kernel(
@@ -44,9 +45,10 @@ def tile_moe_pln_lin_relu_kernel(
         w8_sb = keep.tile([P, E, 4 * N], U8, name="w8_sb", align_bytes=64)
         w4_sb = keep.tile([P, E, 2 * N], U8, name="w4_sb", align_bytes=64)
         w_scales = keep.tile([P, E * N], U8, name="w_scales", align_bytes=64)
-        x_scales = keep.tile([P, 2 * T], U8, name="x_scales", align_bytes=64)
+        x_scales = keep.tile([P, WINDOW], U8, name="x_scales", align_bytes=64)
         slot_scales = keep.tile([P, SLOTS], U8, name="slot_scales", align_bytes=64)
-        x_codes = [keep.tile([P, WINDOW if a == 0 else T], U32, name=f"x_codes{a}", align_bytes=64) for a in range(PASSES)]
+        words = keep.tile([P, T + 2 * EARLY], U32, name="words", align_bytes=64)
+        x_codes = [words[:, T:], words[:, :]]
         slot_codes = [keep.tile([P, (1920, SLOTS)[a]], U32, name=f"slot_codes{a}", align_bytes=64) for a in range(PASSES)]
         bias = keep.tile([P, E], F32, name="bias")
         gates = keep.tile([P, 2, T - TURNED], F32, name="gates")
@@ -54,12 +56,12 @@ def tile_moe_pln_lin_relu_kernel(
         warm = keep.tile([P, 8], F32, name="warm")
 
         identity = keep.tile([P, P], F32, name="identity")
-        nc.gpsimd.memset(warm[:], 0.0)
+        nc.vector.memset(warm[:], 0.0)
         nc.scalar.activation(warm[:, 0:1], warm[:, 1:2], RELU)
-        nc.gpsimd.memset(x_scales[:].bitcast(I32), 0)
-        nc.gpsimd.memset(w_scales[:].bitcast(I32), 0)
+        nc.vector.memset(x_scales[:].bitcast(I32), 0)
+        nc.vector.memset(w_scales[:].bitcast(I32), 0)
         make_identity(nc, identity[:])
-        nc.vector.memset(x_codes[0][:, T:WINDOW].bitcast(I32), 0)
+        nc.vector.memset(words[:, 2 * T :].bitcast(I32), 0)
 
         grouped = [keep.tile([P, T, 4], BF16, name=f"grouped{a}", align_bytes=64) for a in range(PASSES)]
         raw = {}
@@ -138,17 +140,17 @@ def tile_moe_pln_lin_relu_kernel(
             banks.append(psum.tile([P, 2 * C], F32, name=f"acc{len(banks) % 8}"))
             return banks[-1]
 
-        def one_pass(a, acc, s):
-            e = s // C
+        def one_pass(a, acc, lo, hi, stop=False):
+            e = lo // C
             weights = w8_sb[:, e, :].bitcast(FP8X4) if a == 0 else w4_sb[:, e, :].bitcast(FP4X4)
             nc.tensor.matmul_mx(
                 out=acc,
                 lhsT=weights,
                 lhsT_scale=w_scales[FIRST_ROW[a] : P, e * N : (e + 1) * N],
-                rhs=(late_codes[:] if (a, s) == (0, 1920) else slot_codes[a][:, s : s + HALF]).bitcast(FP8X4),
-                rhs_scale=slot_scales[FIRST_ROW[a] : P, s : s + HALF],
+                rhs=(late_codes[:] if (a, lo) == (0, 1920) else slot_codes[a][:, lo:hi]).bitcast(FP8X4),
+                rhs_scale=slot_scales[FIRST_ROW[a] : P, lo:hi],
                 start=(a == 0),
-                stop=(a == 1),
+                stop=stop,
             )
 
         def relu(acc, lo, hi):
@@ -158,11 +160,16 @@ def tile_moe_pln_lin_relu_kernel(
             else:
                 nc.scalar.activation(y[:, lo:hi], acc, RELU, bias=bias[:, e : e + 1])
 
-        def multiply(lo, hi):
-            acc = new_bank()
+        groups = {}
+
+        def open_group(lo, hi):
+            groups[lo] = (new_bank(), hi)
+            one_pass(0, groups[lo][0][:, 0 : hi - lo], lo, hi)
+
+        def close_group(lo):
+            acc, hi = groups[lo]
             for s in range(lo, hi, HALF):
-                for a in (0, 1):
-                    one_pass(a, acc[:, s - lo : s - lo + HALF], s)
+                one_pass(1, acc[:, s - lo : s - lo + HALF], s, s + HALF, stop=(s + HALF == hi))
             relu(acc[:, 0 : hi - lo], lo, hi)
 
         cast(0, 0, 4, 0, 512, 256)
@@ -172,7 +179,7 @@ def tile_moe_pln_lin_relu_kernel(
         quantize(0, 512, 768)
         cast(0, 0, 4, 768, 1024, 160)
         quantize(0, 768, 1024)
-        nc.vector.tensor_copy(slot_codes[0][:, 0:1920], x_codes[0][:].indirect(offs_sb[:, 0 : 1920 // 16]))
+        gather_codes(0, 0, EARLY, 2 * EARLY)
         for lo, hi in ((0, 256), (256, 512), (512, 768), (768, 896), (896, 1024)):
             cast(1, 0, 4, lo, hi, 0)
         quantize(1, 0, 512)
@@ -181,26 +188,16 @@ def tile_moe_pln_lin_relu_kernel(
         quantize(1, 896, 1024)
         late_codes = keep.tile([P, HALF], U32, name="raw1_0_896", align_bytes=64)
         nc.vector.tensor_copy(late_codes[:], x_codes[0][:, 0:T].indirect(offs_sb[:, 1920 // 16 : SLOTS // 16]))
-        gather_scales(0, 1536)
-        for lo, hi in ((0, 768), (768, 1536)):
-            gather_codes(1, lo, hi)
-            for s in range(lo, hi, C):
-                multiply(s, s + C)
-        gather_scales(1536, 2048)
-        pair = new_bank()
-        last = {s: new_bank() for s in (1792, 1920)}
-        one_pass(0, pair[:, 0:HALF], 1536)
-        for s in (1792, 1920):
-            one_pass(0, last[s][:, 0:HALF], s)
-        gather_codes(1, 1536, 1792)
-        one_pass(1, pair[:, 0:HALF], 1536)
-        one_pass(0, pair[:, HALF:C], 1664)
-        one_pass(1, pair[:, HALF:C], 1664)
-        relu(pair[:, 0:C], 1536, 1792)
-        for s in (1792, 1920):
-            gather_codes(1, s, s + HALF)
-            one_pass(1, last[s][:, 0:HALF], s)
-            relu(last[s][:, 0:HALF], s, s + HALF)
+        gather_scales(0, SLOTS)
+        for lo in range(0, SLOTS - C, C):
+            open_group(lo, lo + C)
+        open_group(SLOTS - C, SLOTS - HALF)
+        for lo, hi in ((0, 1024), (1024, 1792), (1792, 2048)):
+            gather_codes(1, lo, hi, 2 * T)
+            for s in range(lo, hi, C if hi < SLOTS else HALF):
+                close_group(s)
+            if lo == 0:
+                open_group(SLOTS - HALF, SLOTS)
 
         picked = [keep.tile([P, T], F32, name=f"picked{g}") for g in range(2)]
         result = keep.tile([P, T], F32, name="result")
@@ -241,8 +238,8 @@ def tile_moe_pln_lin_relu_kernel(
 
         gated(0, 0, 512)
         turn(0, 0, 512)
+        gated(1, 0, 512)
         for lo in (0, 256):
-            gated(1, lo, lo + 256)
             turn(1, lo, lo + 256)
             turn_back_and_store(lo, lo + 256)
         gated(0, 512, 1024)

@@ -175,9 +175,9 @@ def tile_moe_pln_lin_relu_kernel(
         cast(0, 0, 4, 0, 512, 256)
         quantize(0, 0, 256)
         quantize(0, 256, 512)
-        cast(0, 0, 4, 512, 768, 160)
+        cast(0, 0, 4, 512, 768, 128)
+        cast(0, 0, 4, 768, 1024, 176)
         quantize(0, 512, 768)
-        cast(0, 0, 4, 768, 1024, 160)
         quantize(0, 768, 1024)
         gather_codes(0, 0, EARLY, 2 * EARLY)
         for lo, hi in ((0, 256), (256, 512), (512, 768), (768, 896), (896, 1024)):
@@ -189,15 +189,17 @@ def tile_moe_pln_lin_relu_kernel(
         late_codes = keep.tile([P, HALF], U32, name="raw1_0_896", align_bytes=64)
         nc.vector.tensor_copy(late_codes[:], x_codes[0][:, 0:T].indirect(offs_sb[:, 1920 // 16 : SLOTS // 16]))
         gather_scales(0, SLOTS)
-        for lo in range(0, SLOTS - C, C):
-            open_group(lo, lo + C)
-        open_group(SLOTS - C, SLOTS - HALF)
-        for lo, hi in ((0, 1024), (1024, 1792), (1792, 2048)):
-            gather_codes(1, lo, hi, 2 * T)
-            for s in range(lo, hi, C if hi < SLOTS else HALF):
-                close_group(s)
-            if lo == 0:
-                open_group(SLOTS - HALF, SLOTS)
+        spans = [(s, s + C) for s in range(0, SLOTS - 2 * C, C)] + [(s, s + HALF) for s in range(SLOTS - 2 * C, SLOTS, HALF)]
+        for lo, hi in spans[:8]:
+            open_group(lo, hi)
+        for first, last in ((0, 896), (896, 1536), (1536, 1920), (1920, 2048)):
+            gather_codes(1, first, last, 2 * T if first == 0 else T)
+            for lo, hi in spans:
+                if first < hi <= last:
+                    close_group(lo)
+            if first == 0:
+                for lo, hi in spans[8:]:
+                    open_group(lo, hi)
 
         picked = [keep.tile([P, T], F32, name=f"picked{g}") for g in range(2)]
         result = keep.tile([P, T], F32, name="result")

@@ -75,10 +75,13 @@ def tile_moe_pln_lin_relu_kernel(
 
         whole = keep.tile([P, 4, T // 2], F32, name="whole")
 
-        def load_rows(a, j0, j1, lo, hi):
-            raw[a, 0, lo] = whole[:, :, lo - T // 2 : hi - T // 2]
-            nc.sync.dma_start(
-                whole[:, j0:j1, lo - T // 2 : hi - T // 2],
+        front = keep.tile([P, 4, T // 2], F32, name="front")
+
+        def load_rows(a, j0, j1, lo, hi, queue):
+            tile, first = (front, 0) if lo < T // 2 else (whole, T // 2)
+            raw[a, 0, lo] = tile[:, :, lo - first : hi - first]
+            queue.dma_start(
+                tile[:, j0:j1, lo - first : hi - first],
                 xT[512 * a : 512 * (a + 1), lo:hi].rearrange("(p j) t -> p j t", j=4)[:, j0:j1, :],
             )
 
@@ -111,10 +114,11 @@ def tile_moe_pln_lin_relu_kernel(
         def gather_scales(lo, hi):
             nc.vector.tensor_copy(slot_scales[:, lo:hi], x_scales[:].indirect(offs_sb[:, lo // 16 : hi // 16]))
 
-        load(0, 0, 4, 0, 512)
-        load_rows(0, 0, 2, 512, 1024)
-        load_rows(0, 2, 4, 512, 768)
-        load_rows(0, 2, 4, 768, 1024)
+        load_rows(0, 0, 2, 0, 512, nc.sync)
+        load_rows(0, 2, 4, 0, 512, nc.scalar)
+        for j, lo, hi in ((0, 512, 1024), (2, 512, 768), (2, 768, 1024)):
+            load_rows(0, j, j + 1, lo, hi, nc.sync)
+            load_rows(0, j + 1, j + 2, lo, hi, nc.scalar)
         nc.sync.dma_start(offs_sb[:], offs)
         load(1, 0, 4, 0, 256)
         load(1, 0, 4, 256, 512)

@@ -22,13 +22,20 @@ ADD = mybir.AluOpType.add
 MAX = mybir.AluOpType.max
 
 P = 128
-PASSES = 2
+K_PASS = 512
+PASSES = K // K_PASS
+PACK = 4
+LIST_ROWS = 16
+BANKS = 8
 FIRST_ROW = (4, 0)
-HALF = 128
-TURNED = 0
-CHUNK = 256
-WINDOW = 4096
-EARLY = 1920
+HALF = C // 2
+EARLY = SLOTS - HALF
+QUARTER = T // 4
+
+VECTOR_SHARES = (256, 128, 176)
+PASS1_LOADS = ((0, 256), (256, 512), (512, 768), (768, 896), (896, 1024))
+PASS1_QUANTISE = ((0, 512), (512, 768), (768, 896), (896, 1024))
+PASS1_GATHERS = ((0, 896), (896, 1536), (1536, 1920), (1920, 2048))
 
 
 def tile_moe_pln_lin_relu_kernel(
@@ -39,23 +46,25 @@ def tile_moe_pln_lin_relu_kernel(
         keep = ctx.enter_context(tc.tile_pool(name="keep", bufs=1))
         psum = ctx.enter_context(tc.psum_pool(name="psum", bufs=1))
 
-        offs_sb = keep.tile([P, SLOTS // 16], U16, name="offs_sb")
-        pos1_sb = keep.tile([P, T // 16], U16, name="pos1_sb")
-        pos2_sb = keep.tile([P, T // 16], U16, name="pos2_sb")
+        offs_sb = keep.tile([P, SLOTS // LIST_ROWS], U16, name="offs_sb")
+        pos1_sb = keep.tile([P, T // LIST_ROWS], U16, name="pos1_sb")
+        pos2_sb = keep.tile([P, T // LIST_ROWS], U16, name="pos2_sb")
         w8_sb = keep.tile([P, E, 4 * N], U8, name="w8_sb", align_bytes=64)
         w4_sb = keep.tile([P, E, 2 * N], U8, name="w4_sb", align_bytes=64)
         w_scales = keep.tile([P, E * N], U8, name="w_scales", align_bytes=64)
-        x_scales = keep.tile([P, WINDOW], U8, name="x_scales", align_bytes=64)
+        x_scales = keep.tile([P, 2 * SLOTS], U8, name="x_scales", align_bytes=64)
         slot_scales = keep.tile([P, SLOTS], U8, name="slot_scales", align_bytes=64)
         words = keep.tile([P, T + 2 * EARLY], U32, name="words", align_bytes=64)
         x_codes = [words[:, T:], words[:, :]]
-        slot_codes = [keep.tile([P, (1920, SLOTS)[a]], U32, name=f"slot_codes{a}", align_bytes=64) for a in range(PASSES)]
+        slot_codes = [
+            keep.tile([P, (EARLY, SLOTS)[a]], U32, name=f"slot_codes{a}", align_bytes=64) for a in range(PASSES)
+        ]
         bias = keep.tile([P, E], F32, name="bias")
-        gates = keep.tile([P, 2, T - TURNED], F32, name="gates")
+        gates = keep.tile([P, 2, T], F32, name="gates")
         y = keep.tile([P, SLOTS], F32, name="y")
         warm = keep.tile([P, 8], F32, name="warm")
-
         identity = keep.tile([P, P], F32, name="identity")
+
         nc.vector.memset(warm[:], 0.0)
         nc.scalar.activation(warm[:, 0:1], warm[:, 1:2], RELU)
         nc.vector.memset(x_scales[:].bitcast(I32), 0)
@@ -63,43 +72,38 @@ def tile_moe_pln_lin_relu_kernel(
         make_identity(nc, identity[:])
         nc.vector.memset(words[:, 2 * T :].bitcast(I32), 0)
 
-        grouped = [keep.tile([P, T, 4], BF16, name=f"grouped{a}", align_bytes=64) for a in range(PASSES)]
+        grouped = [keep.tile([P, T, PACK], BF16, name=f"grouped{a}", align_bytes=64) for a in range(PASSES)]
         raw = {}
 
-        def load(a, j0, j1, lo, hi):
-            raw[a, j0, lo] = keep.tile([P, j1 - j0, hi - lo], F32, name=f"raw{a}_{j0}_{lo}", align_bytes=64)
-            nc.sync.dma_start(
-                raw[a, j0, lo][:],
-                xT[512 * a : 512 * (a + 1), lo:hi].rearrange("(p j) t -> p j t", j=4)[:, j0:j1, :],
-            )
+        def x_rows(a, lo, hi):
+            return xT[K_PASS * a : K_PASS * (a + 1), lo:hi].rearrange("(p j) t -> p j t", j=PACK)
 
-        whole = keep.tile([P, 4, T // 2], F32, name="whole")
+        second_half = keep.tile([P, PACK, T // 2], F32, name="whole")
+        first_half = keep.tile([P, PACK, T // 2], F32, name="front")
 
-        front = keep.tile([P, 4, T // 2], F32, name="front")
+        def load_pass0(j0, j1, lo, hi):
+            tile, first = (first_half, 0) if lo < T // 2 else (second_half, T // 2)
+            raw[0, lo] = tile[:, :, lo - first : hi - first]
+            middle = (j0 + j1) // 2
+            for queue, r0, r1 in ((nc.sync, j0, middle), (nc.scalar, middle, j1)):
+                queue.dma_start(tile[:, r0:r1, lo - first : hi - first], x_rows(0, lo, hi)[:, r0:r1, :])
 
-        def load_rows(a, j0, j1, lo, hi, queue):
-            tile, first = (front, 0) if lo < T // 2 else (whole, T // 2)
-            raw[a, 0, lo] = tile[:, :, lo - first : hi - first]
-            queue.dma_start(
-                tile[:, j0:j1, lo - first : hi - first],
-                xT[512 * a : 512 * (a + 1), lo:hi].rearrange("(p j) t -> p j t", j=4)[:, j0:j1, :],
-            )
+        def load_pass1(lo, hi):
+            raw[1, lo] = keep.tile([P, PACK, hi - lo], F32, name=f"raw1_0_{lo}", align_bytes=64)
+            nc.sync.dma_start(raw[1, lo][:], x_rows(1, lo, hi))
 
         def scalar_copy(dst, src):
             nc.scalar.activation(dst, src, COPY)
 
-        def interleave(copy, a, j0, j1, first, lo, hi):
+        def interleave(copy, a, first, lo, hi):
             copy(
-                grouped[a][:, lo:hi, j0:j1].rearrange("p (c i) j -> p c j i", i=4),
-                raw[a, j0, first][:, :, lo - first : hi - first].rearrange("p j (c i) -> p c j i", i=4),
+                grouped[a][:, lo:hi, :].rearrange("p (c i) j -> p c j i", i=4),
+                raw[a, first][:, :, lo - first : hi - first].rearrange("p j (c i) -> p c j i", i=4),
             )
 
-        def cast(a, j0, j1, lo, hi, vector_tokens):
-            v = lo + vector_tokens
-            if v > lo:
-                interleave(nc.vector.tensor_copy, a, j0, j1, lo, lo, v)
-            if v < hi:
-                interleave(scalar_copy, a, j0, j1, lo, v, hi)
+        def cast_pass0(lo, hi, vector_tokens):
+            interleave(nc.vector.tensor_copy, 0, lo, lo, lo + vector_tokens)
+            interleave(scalar_copy, 0, lo, lo + vector_tokens, hi)
 
         def quantize(a, lo, hi):
             nc.vector.quantize_mx(
@@ -108,23 +112,19 @@ def tile_moe_pln_lin_relu_kernel(
                 in_=grouped[a][:, lo:hi, :].rearrange("p t j -> p (t j)"),
             )
 
-        def gather_codes(a, lo, hi, window=T):
-            nc.vector.tensor_copy(slot_codes[a][:, lo:hi], x_codes[a][:, 0:window].indirect(offs_sb[:, lo // 16 : hi // 16]))
+        def entries(list_sb, lo, hi):
+            return list_sb[:, lo // LIST_ROWS : hi // LIST_ROWS]
 
-        def gather_scales(lo, hi):
-            nc.vector.tensor_copy(slot_scales[:, lo:hi], x_scales[:].indirect(offs_sb[:, lo // 16 : hi // 16]))
+        def gather_codes(dst, a, lo, hi, window):
+            nc.vector.tensor_copy(dst, x_codes[a][:, 0:window].indirect(entries(offs_sb, lo, hi)))
 
-        load_rows(0, 0, 2, 0, 512, nc.sync)
-        load_rows(0, 2, 4, 0, 512, nc.scalar)
-        for j, lo, hi in ((0, 512, 1024), (2, 512, 768), (2, 768, 1024)):
-            load_rows(0, j, j + 1, lo, hi, nc.sync)
-            load_rows(0, j + 1, j + 2, lo, hi, nc.scalar)
+        load_pass0(0, 4, 0, T // 2)
+        load_pass0(0, 2, T // 2, T)
+        load_pass0(2, 4, T // 2, T - QUARTER)
+        load_pass0(2, 4, T - QUARTER, T)
         nc.sync.dma_start(offs_sb[:], offs)
-        load(1, 0, 4, 0, 256)
-        load(1, 0, 4, 256, 512)
-        load(1, 0, 4, 512, 768)
-        load(1, 0, 4, 768, 896)
-        load(1, 0, 4, 896, 1024)
+        for lo, hi in PASS1_LOADS:
+            load_pass1(lo, hi)
         nc.sync.dma_start(w8_sb[:].bitcast(I32), w8_words[:, 0].rearrange("e p n r -> p e (n r)").bitcast(I32))
         nc.sync.dma_start(w4_sb[:].bitcast(I32), w4_words[:, 0].rearrange("e p m -> p e m").bitcast(I32))
         for source, first in ((w8_scales, FIRST_ROW[0]), (w4_scales, FIRST_ROW[1])):
@@ -136,90 +136,82 @@ def tile_moe_pln_lin_relu_kernel(
         nc.sync.dma_start(bias[:], b)
         nc.sync.dma_start(pos1_sb[:], pos1)
         nc.sync.dma_start(pos2_sb[:], pos2)
-        nc.sync.dma_start(gates[:], gate[:, :, TURNED:T].rearrange("g n t -> n g t"))
+        nc.sync.dma_start(gates[:], gate.rearrange("g n t -> n g t"))
 
         banks = []
 
         def new_bank():
-            banks.append(psum.tile([P, 2 * C], F32, name=f"acc{len(banks) % 8}"))
+            banks.append(psum.tile([P, 2 * C], F32, name=f"acc{len(banks) % BANKS}"))
             return banks[-1]
 
-        def one_pass(a, acc, lo, hi, stop=False):
+        cast_pass0(0, T // 2, VECTOR_SHARES[0])
+        quantize(0, 0, QUARTER)
+        quantize(0, QUARTER, T // 2)
+        cast_pass0(T // 2, T - QUARTER, VECTOR_SHARES[1])
+        cast_pass0(T - QUARTER, T, VECTOR_SHARES[2])
+        quantize(0, T // 2, T - QUARTER)
+        quantize(0, T - QUARTER, T)
+
+        gather_codes(slot_codes[0][:, 0:EARLY], 0, 0, EARLY, 2 * EARLY)
+        for lo, hi in PASS1_LOADS:
+            interleave(scalar_copy, 1, lo, lo, hi)
+        for lo, hi in PASS1_QUANTISE:
+            quantize(1, lo, hi)
+
+        late_codes = keep.tile([P, HALF], U32, name=f"raw1_0_{PASS1_LOADS[-1][0]}", align_bytes=64)
+        gather_codes(late_codes[:], 0, EARLY, SLOTS, T)
+        nc.vector.tensor_copy(slot_scales[:, 0:SLOTS], x_scales[:].indirect(entries(offs_sb, 0, SLOTS)))
+
+        def one_pass(a, acc, lo, hi, stop):
             e = lo // C
             weights = w8_sb[:, e, :].bitcast(FP8X4) if a == 0 else w4_sb[:, e, :].bitcast(FP4X4)
+            codes = late_codes[:] if (a, lo) == (0, EARLY) else slot_codes[a][:, lo:hi]
             nc.tensor.matmul_mx(
                 out=acc,
                 lhsT=weights,
                 lhsT_scale=w_scales[FIRST_ROW[a] : P, e * N : (e + 1) * N],
-                rhs=(late_codes[:] if (a, lo) == (0, 1920) else slot_codes[a][:, lo:hi]).bitcast(FP8X4),
+                rhs=codes.bitcast(FP8X4),
                 rhs_scale=slot_scales[FIRST_ROW[a] : P, lo:hi],
                 start=(a == 0),
                 stop=stop,
             )
 
-        def relu(acc, lo, hi):
-            e = lo // C
-            if hi == SLOTS - HALF:
-                nc.vector.tensor_scalar(y[:, lo:hi], acc, bias[:, e : e + 1], 0.0, ADD, MAX)
-            else:
-                nc.scalar.activation(y[:, lo:hi], acc, RELU, bias=bias[:, e : e + 1])
-
-        groups = {}
+        groups = [(s, s + C) for s in range(0, SLOTS - 2 * C, C)]
+        groups = groups + [(s, s + HALF) for s in range(SLOTS - 2 * C, SLOTS, HALF)]
+        sums = {}
 
         def open_group(lo, hi):
-            groups[lo] = (new_bank(), hi)
-            one_pass(0, groups[lo][0][:, 0 : hi - lo], lo, hi)
+            sums[lo] = new_bank()
+            one_pass(0, sums[lo][:, 0 : hi - lo], lo, hi, False)
 
-        def close_group(lo):
-            acc, hi = groups[lo]
+        def close_group(lo, hi):
             for s in range(lo, hi, HALF):
-                one_pass(1, acc[:, s - lo : s - lo + HALF], s, s + HALF, stop=(s + HALF == hi))
-            relu(acc[:, 0 : hi - lo], lo, hi)
+                one_pass(1, sums[lo][:, s - lo : s - lo + HALF], s, s + HALF, s + HALF == hi)
+            column = bias[:, lo // C : lo // C + 1]
+            if hi == SLOTS - HALF:
+                nc.vector.tensor_scalar(y[:, lo:hi], sums[lo][:, 0 : hi - lo], column, 0.0, ADD, MAX)
+            else:
+                nc.scalar.activation(y[:, lo:hi], sums[lo][:, 0 : hi - lo], RELU, bias=column)
 
-        cast(0, 0, 4, 0, 512, 256)
-        quantize(0, 0, 256)
-        quantize(0, 256, 512)
-        cast(0, 0, 4, 512, 768, 128)
-        cast(0, 0, 4, 768, 1024, 176)
-        quantize(0, 512, 768)
-        quantize(0, 768, 1024)
-        gather_codes(0, 0, EARLY, 2 * EARLY)
-        for lo, hi in ((0, 256), (256, 512), (512, 768), (768, 896), (896, 1024)):
-            cast(1, 0, 4, lo, hi, 0)
-        quantize(1, 0, 512)
-        quantize(1, 512, 768)
-        quantize(1, 768, 896)
-        quantize(1, 896, 1024)
-        late_codes = keep.tile([P, HALF], U32, name="raw1_0_896", align_bytes=64)
-        nc.vector.tensor_copy(late_codes[:], x_codes[0][:, 0:T].indirect(offs_sb[:, 1920 // 16 : SLOTS // 16]))
-        gather_scales(0, SLOTS)
-        spans = [(s, s + C) for s in range(0, SLOTS - 2 * C, C)] + [(s, s + HALF) for s in range(SLOTS - 2 * C, SLOTS, HALF)]
-        for lo, hi in spans[:8]:
+        for lo, hi in groups[:BANKS]:
             open_group(lo, hi)
-        for first, last in ((0, 896), (896, 1536), (1536, 1920), (1920, 2048)):
-            gather_codes(1, first, last, 2 * T if first == 0 else T)
-            for lo, hi in spans:
+        for first, last in PASS1_GATHERS:
+            gather_codes(slot_codes[1][:, first:last], 1, first, last, 2 * T if first == 0 else T)
+            for lo, hi in groups:
                 if first < hi <= last:
-                    close_group(lo)
+                    close_group(lo, hi)
             if first == 0:
-                for lo, hi in spans[8:]:
+                for lo, hi in groups[BANKS:]:
                     open_group(lo, hi)
 
         picked = [keep.tile([P, T], F32, name=f"picked{g}") for g in range(2)]
         result = keep.tile([P, T], F32, name="result")
+        turned_sum = keep.tile([P, T], F32, name="turned_sum")
         pos_sb = (pos1_sb, pos2_sb)
-
-        def looked_up(g, lo, hi):
-            return y[:].indirect(pos_sb[g][:, lo // 16 : hi // 16])
+        turned = {}
 
         def gated(g, lo, hi):
-            nc.vector.tensor_tensor(
-                picked[g][:, lo:hi], looked_up(g, lo, hi), gates[:, g, lo - TURNED : hi - TURNED], MULT
-            )
-
-        turned_sum = keep.tile([P, T], F32, name="turned_sum")
-
-        turned = {}
+            nc.vector.tensor_tensor(picked[g][:, lo:hi], y[:].indirect(entries(pos_sb[g], lo, hi)), gates[:, g, lo:hi], MULT)
 
         def turn(g, lo, hi):
             for s in range(lo, hi, P):
@@ -242,14 +234,14 @@ def tile_moe_pln_lin_relu_kernel(
             nc.vector.tensor_add(result[:, lo:hi], picked[0][:, lo:hi], picked[1][:, lo:hi])
             nc.sync.dma_start(out[:, lo:hi], result[:, lo:hi])
 
-        gated(0, 0, 512)
-        turn(0, 0, 512)
-        gated(1, 0, 512)
-        for lo in (0, 256):
-            turn(1, lo, lo + 256)
-            turn_back_and_store(lo, lo + 256)
-        gated(0, 512, 1024)
-        gated(1, 512, 768)
-        gated(1, 768, 1024)
-        add_and_store(512, 768)
-        add_and_store(768, 1024)
+        gated(0, 0, T // 2)
+        turn(0, 0, T // 2)
+        for lo in (0, QUARTER):
+            gated(1, lo, lo + QUARTER)
+            turn(1, lo, lo + QUARTER)
+            turn_back_and_store(lo, lo + QUARTER)
+        gated(0, T // 2, T)
+        gated(1, T // 2, T - QUARTER)
+        gated(1, T - QUARTER, T)
+        add_and_store(T // 2, T - QUARTER)
+        add_and_store(T - QUARTER, T)

@@ -31,6 +31,7 @@ FIRST_ROW = (4, 0)
 HALF = C // 2
 EARLY = SLOTS - HALF
 QUARTER = T // 4
+BURST = 256
 
 VECTOR_SHARES = (256, 128, 176)
 PASS1_LOADS = ((0, 256), (256, 512), (512, 768), (768, 896), (896, 1024))
@@ -46,11 +47,11 @@ def tile_moe_pln_lin_relu_kernel(
         keep = ctx.enter_context(tc.tile_pool(name="keep", bufs=1))
         psum = ctx.enter_context(tc.psum_pool(name="psum", bufs=1))
 
-        offs_sb = keep.tile([P, SLOTS // LIST_ROWS], U16, name="offs_sb")
+        offs_sb = keep.tile([P, SLOTS // LIST_ROWS], U16, name="offs_sb", align_bytes=BURST)
         pos1_sb = keep.tile([P, T // LIST_ROWS], U16, name="pos1_sb")
         pos2_sb = keep.tile([P, T // LIST_ROWS], U16, name="pos2_sb")
-        w8_sb = keep.tile([P, E, 4 * N], U8, name="w8_sb", align_bytes=64)
-        w4_sb = keep.tile([P, E, 2 * N], U8, name="w4_sb", align_bytes=64)
+        w8_sb = keep.tile([P, E, 4 * N], U8, name="w8_sb", align_bytes=BURST)
+        w4_sb = keep.tile([P, E, 2 * N], U8, name="w4_sb", align_bytes=BURST)
         w_scales = keep.tile([P, E * N], U8, name="w_scales", align_bytes=64)
         x_scales = keep.tile([P, 2 * SLOTS], U8, name="x_scales", align_bytes=64)
         slot_scales = keep.tile([P, SLOTS], U8, name="slot_scales", align_bytes=64)
@@ -60,7 +61,7 @@ def tile_moe_pln_lin_relu_kernel(
             keep.tile([P, (EARLY, SLOTS)[a]], U32, name=f"slot_codes{a}", align_bytes=64) for a in range(PASSES)
         ]
         bias = keep.tile([P, E], F32, name="bias")
-        gates = keep.tile([P, 2, T], F32, name="gates")
+        gates = keep.tile([P, 2, T], F32, name="gates", align_bytes=BURST)
         y = keep.tile([P, SLOTS], F32, name="y")
         warm = keep.tile([P, 8], F32, name="warm")
         identity = keep.tile([P, P], F32, name="identity")
@@ -78,8 +79,8 @@ def tile_moe_pln_lin_relu_kernel(
         def x_rows(a, lo, hi):
             return xT[K_PASS * a : K_PASS * (a + 1), lo:hi].rearrange("(p j) t -> p j t", j=PACK)
 
-        second_half = keep.tile([P, PACK, T // 2], F32, name="whole")
-        first_half = keep.tile([P, PACK, T // 2], F32, name="front")
+        second_half = keep.tile([P, PACK, T // 2], F32, name="whole", align_bytes=BURST)
+        first_half = keep.tile([P, PACK, T // 2], F32, name="front", align_bytes=BURST)
 
         def load_pass0(j0, j1, lo, hi):
             tile, first = (first_half, 0) if lo < T // 2 else (second_half, T // 2)
@@ -89,7 +90,7 @@ def tile_moe_pln_lin_relu_kernel(
                 queue.dma_start(tile[:, r0:r1, lo - first : hi - first], x_rows(0, lo, hi)[:, r0:r1, :])
 
         def load_pass1(lo, hi):
-            raw[1, lo] = keep.tile([P, PACK, hi - lo], F32, name=f"raw1_0_{lo}", align_bytes=64)
+            raw[1, lo] = keep.tile([P, PACK, hi - lo], F32, name=f"raw1_0_{lo}", align_bytes=BURST)
             nc.sync.dma_start(raw[1, lo][:], x_rows(1, lo, hi))
 
         def scalar_copy(dst, src):
@@ -158,7 +159,7 @@ def tile_moe_pln_lin_relu_kernel(
         for lo, hi in PASS1_QUANTISE:
             quantize(1, lo, hi)
 
-        late_codes = keep.tile([P, HALF], U32, name=f"raw1_0_{PASS1_LOADS[-1][0]}", align_bytes=64)
+        late_codes = keep.tile([P, HALF], U32, name=f"raw1_0_{PASS1_LOADS[-1][0]}", align_bytes=BURST)
         gather_codes(late_codes[:], 0, EARLY, SLOTS, T)
         nc.vector.tensor_copy(slot_scales[:, 0:SLOTS], x_scales[:].indirect(entries(offs_sb, 0, SLOTS)))
 
@@ -205,7 +206,7 @@ def tile_moe_pln_lin_relu_kernel(
                     open_group(lo, hi)
 
         picked = [keep.tile([P, T], F32, name=f"picked{g}") for g in range(2)]
-        result = keep.tile([P, T], F32, name="result")
+        result = keep.tile([P, T], F32, name="result", align_bytes=BURST)
         turned_sum = keep.tile([P, T], F32, name="turned_sum")
         pos_sb = (pos1_sb, pos2_sb)
         turned = {}

@@ -1,7 +1,6 @@
 from contextlib import ExitStack
 
 import concourse.mybir as mybir
-from concourse.masks import make_identity
 
 K, T, E, C, N = 1024, 1024, 8, 256, 128
 SLOTS = E * C
@@ -64,13 +63,11 @@ def tile_moe_pln_lin_relu_kernel(
         gates = keep.tile([P, 2, T], F32, name="gates", align_bytes=BURST)
         y = keep.tile([P, SLOTS], F32, name="y")
         warm = keep.tile([P, 8], F32, name="warm")
-        identity = keep.tile([P, P], F32, name="identity")
 
         nc.vector.memset(warm[:], 0.0)
         nc.scalar.activation(warm[:, 0:1], warm[:, 1:2], RELU)
         nc.vector.memset(x_scales[:].bitcast(I32), 0)
         nc.vector.memset(w_scales[:].bitcast(I32), 0)
-        make_identity(nc, identity[:])
         nc.vector.memset(words[:, 2 * T :].bitcast(I32), 0)
 
         grouped = [keep.tile([P, T, PACK], BF16, name=f"grouped{a}", align_bytes=64) for a in range(PASSES)]
@@ -205,44 +202,36 @@ def tile_moe_pln_lin_relu_kernel(
                 for lo, hi in groups[BANKS:]:
                     open_group(lo, hi)
 
-        picked = [keep.tile([P, T], F32, name=f"picked{g}") for g in range(2)]
+        fetched = keep.tile([P, 2, T], F32, name="fetched")
+        products = keep.tile([P, 2, T], F32, name="products")
         result = keep.tile([P, T], F32, name="result", align_bytes=BURST)
-        turned_sum = keep.tile([P, T], F32, name="turned_sum")
         pos_sb = (pos1_sb, pos2_sb)
-        turned = {}
 
-        def gated(g, lo, hi):
-            nc.vector.tensor_tensor(picked[g][:, lo:hi], y[:].indirect(entries(pos_sb[g], lo, hi)), gates[:, g, lo:hi], MULT)
+        def fetch(g, lo, hi):
+            nc.scalar.activation(fetched[:, g, lo:hi], y[:].indirect(entries(pos_sb[g], lo, hi)), COPY)
 
-        def turn(g, lo, hi):
-            for s in range(lo, hi, P):
-                if g == 0:
-                    turned[s] = new_bank()
-                nc.tensor.matmul(
-                    turned[s][:, 0:P], picked[g][:, s : s + P], identity[:], start=(g == 0), stop=(g == 1), is_transpose=True
-                )
-                if g == 1:
-                    nc.scalar.activation(turned_sum[:, s : s + P], turned[s][:, 0:P], COPY)
+        def fetch_gated(g, lo, hi):
+            nc.vector.tensor_tensor(products[:, g, lo:hi], y[:].indirect(entries(pos_sb[g], lo, hi)), gates[:, g, lo:hi], MULT)
 
-        def turn_back_and_store(lo, hi):
-            back = new_bank()
-            for s in range(lo, hi, P):
-                nc.tensor.transpose(back[:, s - lo : s - lo + P], turned_sum[:, s : s + P], identity[:])
-            nc.scalar.activation(result[:, lo:hi], back[:, 0 : hi - lo], COPY)
-            nc.scalar.dma_start(out[:, lo:hi], result[:, lo:hi])
+        def gate_fetched(g, lo, hi):
+            nc.vector.tensor_tensor(products[:, g, lo:hi], fetched[:, g, lo:hi], gates[:, g, lo:hi], MULT)
 
-        def add_and_store(lo, hi):
-            nc.vector.tensor_add(result[:, lo:hi], picked[0][:, lo:hi], picked[1][:, lo:hi])
-            nc.sync.dma_start(out[:, lo:hi], result[:, lo:hi])
+        def finish(lo, hi, stores):
+            halves = ((lo, (lo + hi) // 2), ((lo + hi) // 2, hi))
+            for a, z in halves:
+                gate_fetched(1, a, z)
+            for a, z in halves:
+                nc.vector.tensor_add(result[:, a:z], products[:, 0, a:z], products[:, 1, a:z])
+                if stores == 2:
+                    nc.sync.dma_start(out[:, a:z], result[:, a:z])
+            if stores == 1:
+                nc.sync.dma_start(out[:, lo:hi], result[:, lo:hi])
 
-        gated(0, 0, T // 2)
-        turn(0, 0, T // 2)
-        for lo in (0, QUARTER):
-            gated(1, lo, lo + QUARTER)
-            turn(1, lo, lo + QUARTER)
-            turn_back_and_store(lo, lo + QUARTER)
-        gated(0, T // 2, T)
-        gated(1, T // 2, T - QUARTER)
-        gated(1, T - QUARTER, T)
-        add_and_store(T // 2, T - QUARTER)
-        add_and_store(T - QUARTER, T)
+        fetch_gated(0, 0, 512)
+        fetch(1, 0, 512)
+        finish(0, 512, 2)
+        for lo, hi in ((512, 832), (832, 1024)):
+            fetch(0, lo, hi)
+            fetch(1, lo, hi)
+            gate_fetched(0, lo, hi)
+            finish(lo, hi, 1)

@@ -1,6 +1,7 @@
 from contextlib import ExitStack
 
 import concourse.mybir as mybir
+from concourse.masks import make_identity
 
 K, T, E, C, N = 1024, 1024, 8, 256, 128
 SLOTS = E * C
@@ -29,6 +30,7 @@ BANKS = 8
 FIRST_ROW = (4, 0)
 HALF = C // 2
 EARLY = SLOTS - HALF
+FUSED = 768
 QUARTER = T // 4
 BURST = 256
 
@@ -60,14 +62,19 @@ def tile_moe_pln_lin_relu_kernel(
             keep.tile([P, (EARLY, SLOTS)[a]], U32, name=f"slot_codes{a}", align_bytes=64) for a in range(PASSES)
         ]
         bias = keep.tile([P, E], F32, name="bias")
-        gates = keep.tile([P, 2, T], F32, name="gates", align_bytes=BURST)
+        gates = keep.tile([P, FUSED], F32, name="gates", align_bytes=BURST)
+        gate_rows = keep.tile([P, P], F32, name="gate_rows", align_bytes=BURST)
+        gate_columns = keep.tile([P, 2 * T // P], F32, name="gate_columns")
         y = keep.tile([P, SLOTS], F32, name="y")
         warm = keep.tile([P, 8], F32, name="warm")
+        identity = keep.tile([P, P], F32, name="identity")
 
         nc.vector.memset(warm[:], 0.0)
         nc.scalar.activation(warm[:, 0:1], warm[:, 1:2], RELU)
         nc.vector.memset(x_scales[:].bitcast(I32), 0)
         nc.vector.memset(w_scales[:].bitcast(I32), 0)
+        make_identity(nc, identity[:])
+        nc.vector.memset(gate_rows[:], 0.0)
         nc.vector.memset(words[:, 2 * T :].bitcast(I32), 0)
 
         grouped = [keep.tile([P, T, PACK], BF16, name=f"grouped{a}", align_bytes=64) for a in range(PASSES)]
@@ -124,6 +131,8 @@ def tile_moe_pln_lin_relu_kernel(
         for lo, hi in PASS1_LOADS:
             load_pass1(lo, hi)
         nc.sync.dma_start(w8_sb[:].bitcast(I32), w8_words[:, 0].rearrange("e p n r -> p e (n r)").bitcast(I32))
+        for g in range(2):
+            nc.sync.dma_start(gate_rows[8 * g : 8 * g + 8, :], gate[g, 0, :].rearrange("(b p) -> b p", p=P))
         nc.sync.dma_start(w4_sb[:].bitcast(I32), w4_words[:, 0].rearrange("e p m -> p e m").bitcast(I32))
         for source, first in ((w8_scales, FIRST_ROW[0]), (w4_scales, FIRST_ROW[1])):
             for q in range(4):
@@ -134,13 +143,17 @@ def tile_moe_pln_lin_relu_kernel(
         nc.sync.dma_start(bias[:], b)
         nc.sync.dma_start(pos1_sb[:], pos1)
         nc.sync.dma_start(pos2_sb[:], pos2)
-        nc.sync.dma_start(gates[:], gate.rearrange("g n t -> n g t"))
+        nc.sync.dma_start(gates[:], gate[0, :, 0:FUSED])
 
         banks = []
 
         def new_bank():
             banks.append(psum.tile([P, 2 * C], F32, name=f"acc{len(banks) % BANKS}"))
             return banks[-1]
+
+        turned_rows = new_bank()
+        nc.tensor.transpose(turned_rows[:, 0:P], gate_rows[:], identity[:])
+        nc.scalar.activation(gate_columns[:], turned_rows[:, 0 : 2 * T // P], COPY)
 
         cast_pass0(0, T // 2, VECTOR_SHARES[0])
         quantize(0, 0, QUARTER)
@@ -211,27 +224,44 @@ def tile_moe_pln_lin_relu_kernel(
             nc.scalar.activation(fetched[:, g, lo:hi], y[:].indirect(entries(pos_sb[g], lo, hi)), COPY)
 
         def fetch_gated(g, lo, hi):
-            nc.vector.tensor_tensor(products[:, g, lo:hi], y[:].indirect(entries(pos_sb[g], lo, hi)), gates[:, g, lo:hi], MULT)
+            nc.vector.tensor_tensor(products[:, g, lo:hi], y[:].indirect(entries(pos_sb[g], lo, hi)), gates[:, lo:hi], MULT)
 
-        def gate_fetched(g, lo, hi):
-            nc.vector.tensor_tensor(products[:, g, lo:hi], fetched[:, g, lo:hi], gates[:, g, lo:hi], MULT)
+        spread = {}
+        for g, first, last in ((1, 0, T // 2), (1, T // 2, T), (0, FUSED, T)):
+            bank = new_bank()
+            for s in range(first, last, P):
+                block = g * T // P + s // P
+                nc.tensor.transpose(bank[:, s - first : s - first + P], gate_columns[:, block : block + 1].to_broadcast([P, P]), identity[:])
+                spread[g, s] = (bank, first)
 
-        def finish(lo, hi, stores):
-            halves = ((lo, (lo + hi) // 2), ((lo + hi) // 2, hi))
-            for a, z in halves:
-                gate_fetched(1, a, z)
-            for a, z in halves:
-                nc.vector.tensor_add(result[:, a:z], products[:, 0, a:z], products[:, 1, a:z])
-                if stores == 2:
-                    nc.sync.dma_start(out[:, a:z], result[:, a:z])
-            if stores == 1:
-                nc.sync.dma_start(out[:, lo:hi], result[:, lo:hi])
+        def gate_fetched(g, g1, lo, hi):
+            bank, first = spread[g, lo - lo % P]
+            nc.vector.tensor_tensor(products[:, g, lo:hi], fetched[:, g, lo:hi], bank[:, lo - first : hi - first], MULT)
 
-        fetch_gated(0, 0, 512)
+        def add_aside(lo, hi):
+            nc.gpsimd.tensor_tensor(result[:, lo:hi], products[:, 0, lo:hi], products[:, 1, lo:hi], ADD)
+
+        def add(lo, hi):
+            nc.vector.tensor_add(result[:, lo:hi], products[:, 0, lo:hi], products[:, 1, lo:hi])
+
+        def store(lo, hi):
+            nc.sync.dma_start(out[:, lo:hi], result[:, lo:hi])
+
         fetch(1, 0, 512)
-        finish(0, 512, 2)
-        for lo, hi in ((512, 832), (832, 1024)):
-            fetch(0, lo, hi)
-            fetch(1, lo, hi)
-            gate_fetched(0, lo, hi)
-            finish(lo, hi, 1)
+        fetch(1, 512, 768)
+        fetch(0, 768, 1024)
+        fetch(1, 768, 1024)
+        fetch_gated(0, 0, 768)
+        gate_fetched(1, 2, 0, 256)
+        gate_fetched(1, 2, 256, 512)
+        add_aside(0, 256)
+        store(0, 256)
+        add_aside(256, 512)
+        store(256, 512)
+        gate_fetched(1, 2, 512, 768)
+        gate_fetched(0, 1, 768, 1024)
+        gate_fetched(1, 2, 768, 1024)
+        add(512, 768)
+        store(512, 768)
+        add(768, 1024)
+        store(768, 1024)

@@ -130,10 +130,14 @@ def tile_moe_pln_lin_relu_kernel(
         nc.sync.dma_start(offs_sb[:], offs)
         for lo, hi in PASS1_LOADS:
             load_pass1(lo, hi)
-        nc.sync.dma_start(w8_sb[:].bitcast(I32), w8_words[:, 0].rearrange("e p n r -> p e (n r)").bitcast(I32))
+        for e in (0, E // 2):
+            experts = slice(e, e + E // 2)
+            nc.sync.dma_start(w8_sb[:, experts, :].bitcast(I32), w8_words[experts, 0].rearrange("e p n r -> p e (n r)").bitcast(I32))
         for g in range(2):
             nc.sync.dma_start(gate_rows[8 * g : 8 * g + 8, :], gate[g, 0, :].rearrange("(b p) -> b p", p=P))
-        nc.sync.dma_start(w4_sb[:].bitcast(I32), w4_words[:, 0].rearrange("e p m -> p e m").bitcast(I32))
+        for e in (0, E // 2):
+            experts = slice(e, e + E // 2)
+            nc.sync.dma_start(w4_sb[:, experts, :].bitcast(I32), w4_words[experts, 0].rearrange("e p m -> p e m").bitcast(I32))
         for source, first in ((w8_scales, FIRST_ROW[0]), (w4_scales, FIRST_ROW[1])):
             for q in range(4):
                 nc.sync.dma_start(

@@ -130,13 +130,13 @@ def tile_moe_pln_lin_relu_kernel(
         nc.sync.dma_start(offs_sb[:], offs)
         for lo, hi in PASS1_LOADS:
             load_pass1(lo, hi)
-        for e in (0, E // 2):
-            experts = slice(e, e + E // 2)
+        for e in range(0, E, 2):
+            experts = slice(e, e + 2)
             nc.sync.dma_start(w8_sb[:, experts, :].bitcast(I32), w8_words[experts, 0].rearrange("e p n r -> p e (n r)").bitcast(I32))
         for g in range(2):
             nc.sync.dma_start(gate_rows[8 * g : 8 * g + 8, :], gate[g, 0, :].rearrange("(b p) -> b p", p=P))
-        for e in (0, E // 2):
-            experts = slice(e, e + E // 2)
+        for e in range(0, E, 2):
+            experts = slice(e, e + 2)
             nc.sync.dma_start(w4_sb[:, experts, :].bitcast(I32), w4_words[experts, 0].rearrange("e p m -> p e m").bitcast(I32))
         for source, first in ((w8_scales, FIRST_ROW[0]), (w4_scales, FIRST_ROW[1])):
             for q in range(4):
@@ -147,7 +147,8 @@ def tile_moe_pln_lin_relu_kernel(
         nc.sync.dma_start(bias[:], b)
         nc.sync.dma_start(pos1_sb[:], pos1)
         nc.sync.dma_start(pos2_sb[:], pos2)
-        nc.sync.dma_start(gates[:], gate[0, :, 0:FUSED])
+        for lo, hi in ((0, T // 2), (T // 2, FUSED)):
+            nc.sync.dma_start(gates[:, lo:hi], gate[0, :, lo:hi])
 
         banks = []
 
@@ -260,12 +261,12 @@ def tile_moe_pln_lin_relu_kernel(
         gate_fetched(1, 2, 256, 512)
         add_aside(0, 256)
         store(0, 256)
-        add_aside(256, 512)
-        store(256, 512)
         gate_fetched(1, 2, 512, 768)
         gate_fetched(0, 1, 768, 1024)
-        gate_fetched(1, 2, 768, 1024)
-        add(512, 768)
-        store(512, 768)
-        add(768, 1024)
+        add(256, 768)
+        store(256, 768)
+        gate_fetched(1, 2, 768, 896)
+        gate_fetched(1, 2, 896, 1024)
+        add(768, 896)
+        add(896, 1024)
         store(768, 1024)

@@ -30,8 +30,10 @@ BANKS = 8
 FIRST_ROW = (4, 0)
 HALF = C // 2
 EARLY = SLOTS - HALF
-FUSED = 768
 QUARTER = T // 4
+FUSED = 3 * QUARTER
+SPREAD = ((1, 0, T // 2), (1, T // 2, T), (0, FUSED, T))
+EXPERTS_A_LOAD = 2
 BURST = 256
 
 VECTOR_SHARES = (256, 128, 176)
@@ -63,8 +65,9 @@ def tile_moe_pln_lin_relu_kernel(
         ]
         bias = keep.tile([P, E], F32, name="bias")
         gates = keep.tile([P, FUSED], F32, name="gates", align_bytes=BURST)
+        gate_blocks = [(g, s) for g, first, last in SPREAD for s in range(first, last, P)]
         gate_rows = keep.tile([P, P], F32, name="gate_rows", align_bytes=BURST)
-        gate_columns = keep.tile([P, 2 * T // P], F32, name="gate_columns")
+        gate_columns = keep.tile([P, len(gate_blocks)], F32, name="gate_columns")
         y = keep.tile([P, SLOTS], F32, name="y")
         warm = keep.tile([P, 8], F32, name="warm")
         identity = keep.tile([P, P], F32, name="identity")
@@ -130,14 +133,21 @@ def tile_moe_pln_lin_relu_kernel(
         nc.sync.dma_start(offs_sb[:], offs)
         for lo, hi in PASS1_LOADS:
             load_pass1(lo, hi)
-        for e in range(0, E, 2):
-            experts = slice(e, e + 2)
-            nc.sync.dma_start(w8_sb[:, experts, :].bitcast(I32), w8_words[experts, 0].rearrange("e p n r -> p e (n r)").bitcast(I32))
-        for g in range(2):
-            nc.sync.dma_start(gate_rows[8 * g : 8 * g + 8, :], gate[g, 0, :].rearrange("(b p) -> b p", p=P))
-        for e in range(0, E, 2):
-            experts = slice(e, e + 2)
-            nc.sync.dma_start(w4_sb[:, experts, :].bitcast(I32), w4_words[experts, 0].rearrange("e p m -> p e m").bitcast(I32))
+        for e in range(0, E, EXPERTS_A_LOAD):
+            experts = slice(e, e + EXPERTS_A_LOAD)
+            nc.sync.dma_start(
+                w8_sb[:, experts, :].bitcast(I32), w8_words[experts, 0].rearrange("e p n r -> p e (n r)").bitcast(I32)
+            )
+        for g, first in ((0, FUSED), (1, 0)):
+            row = gate_blocks.index((g, first))
+            nc.sync.dma_start(
+                gate_rows[row : row + (T - first) // P, :], gate[g, 0, first:T].rearrange("(r s) -> r s", s=P)
+            )
+        for e in range(0, E, EXPERTS_A_LOAD):
+            experts = slice(e, e + EXPERTS_A_LOAD)
+            nc.sync.dma_start(
+                w4_sb[:, experts, :].bitcast(I32), w4_words[experts, 0].rearrange("e p m -> p e m").bitcast(I32)
+            )
         for source, first in ((w8_scales, FIRST_ROW[0]), (w4_scales, FIRST_ROW[1])):
             for q in range(4):
                 nc.sync.dma_start(
@@ -158,7 +168,7 @@ def tile_moe_pln_lin_relu_kernel(
 
         turned_rows = new_bank()
         nc.tensor.transpose(turned_rows[:, 0:P], gate_rows[:], identity[:])
-        nc.scalar.activation(gate_columns[:], turned_rows[:, 0 : 2 * T // P], COPY)
+        scalar_copy(gate_columns[:], turned_rows[:, 0 : len(gate_blocks)])
 
         cast_pass0(0, T // 2, VECTOR_SHARES[0])
         quantize(0, 0, QUARTER)
@@ -225,48 +235,45 @@ def tile_moe_pln_lin_relu_kernel(
         result = keep.tile([P, T], F32, name="result", align_bytes=BURST)
         pos_sb = (pos1_sb, pos2_sb)
 
-        def fetch(g, lo, hi):
-            nc.scalar.activation(fetched[:, g, lo:hi], y[:].indirect(entries(pos_sb[g], lo, hi)), COPY)
-
-        def fetch_gated(g, lo, hi):
-            nc.vector.tensor_tensor(products[:, g, lo:hi], y[:].indirect(entries(pos_sb[g], lo, hi)), gates[:, lo:hi], MULT)
-
         spread = {}
-        for g, first, last in ((1, 0, T // 2), (1, T // 2, T), (0, FUSED, T)):
+        for g, first, last in SPREAD:
             bank = new_bank()
             for s in range(first, last, P):
-                block = g * T // P + s // P
-                nc.tensor.transpose(bank[:, s - first : s - first + P], gate_columns[:, block : block + 1].to_broadcast([P, P]), identity[:])
+                r = gate_blocks.index((g, s))
+                nc.tensor.transpose(
+                    bank[:, s - first : s - first + P], gate_columns[:, r : r + 1].to_broadcast([P, P]), identity[:]
+                )
                 spread[g, s] = (bank, first)
 
-        def gate_fetched(g, g1, lo, hi):
-            bank, first = spread[g, lo - lo % P]
+        def looked_up(g, lo, hi):
+            return y[:].indirect(entries(pos_sb[g], lo, hi))
+
+        def multiply(g, lo, hi):
+            bank, first = spread[g, lo]
             nc.vector.tensor_tensor(products[:, g, lo:hi], fetched[:, g, lo:hi], bank[:, lo - first : hi - first], MULT)
 
-        def add_aside(lo, hi):
-            nc.gpsimd.tensor_tensor(result[:, lo:hi], products[:, 0, lo:hi], products[:, 1, lo:hi], ADD)
-
-        def add(lo, hi):
-            nc.vector.tensor_add(result[:, lo:hi], products[:, 0, lo:hi], products[:, 1, lo:hi])
+        def add(engine, lo, hi):
+            engine.tensor_tensor(result[:, lo:hi], products[:, 0, lo:hi], products[:, 1, lo:hi], ADD)
 
         def store(lo, hi):
             nc.sync.dma_start(out[:, lo:hi], result[:, lo:hi])
 
-        fetch(1, 0, 512)
-        fetch(1, 512, 768)
-        fetch(0, 768, 1024)
-        fetch(1, 768, 1024)
-        fetch_gated(0, 0, 768)
-        gate_fetched(1, 2, 0, 256)
-        gate_fetched(1, 2, 256, 512)
-        add_aside(0, 256)
-        store(0, 256)
-        gate_fetched(1, 2, 512, 768)
-        gate_fetched(0, 1, 768, 1024)
-        add(256, 768)
-        store(256, 768)
-        gate_fetched(1, 2, 768, 896)
-        gate_fetched(1, 2, 896, 1024)
-        add(768, 896)
-        add(896, 1024)
-        store(768, 1024)
+        for g, lo, hi in ((1, 0, T // 2), (1, T // 2, FUSED), (0, FUSED, T), (1, FUSED, T)):
+            scalar_copy(fetched[:, g, lo:hi], looked_up(g, lo, hi))
+        nc.vector.tensor_tensor(products[:, 0, 0:FUSED], looked_up(0, 0, FUSED), gates[:], MULT)
+
+        multiply(1, 0, QUARTER)
+        multiply(1, QUARTER, T // 2)
+        add(nc.gpsimd, 0, QUARTER)
+        store(0, QUARTER)
+        multiply(1, T // 2, FUSED)
+        multiply(0, FUSED, T)
+        add(nc.vector, QUARTER, FUSED)
+        store(QUARTER, FUSED)
+
+        halves = ((FUSED, T - P), (T - P, T))
+        for lo, hi in halves:
+            multiply(1, lo, hi)
+        for lo, hi in halves:
+            add(nc.vector, lo, hi)
+        store(FUSED, T)

@@ -32,11 +32,12 @@ HALF = C // 2
 EARLY = SLOTS - HALF
 QUARTER = T // 4
 FUSED = 3 * QUARTER
+SPACER = FUSED - 192
 SPREAD = ((1, 0, T // 2), (1, T // 2, T), (0, FUSED, T))
 EXPERTS_A_LOAD = 2
 BURST = 256
 
-VECTOR_SHARES = (256, 128, 176)
+VECTOR_SHARES = (256, 160, 160)
 PASS1_LOADS = ((0, 256), (256, 512), (512, 768), (768, 896), (896, 1024))
 PASS1_QUANTISE = ((0, 512), (512, 768), (768, 896), (896, 1024))
 PASS1_GATHERS = ((0, 896), (896, 1536), (1536, 1920), (1920, 2048))
@@ -157,8 +158,7 @@ def tile_moe_pln_lin_relu_kernel(
         nc.sync.dma_start(bias[:], b)
         nc.sync.dma_start(pos1_sb[:], pos1)
         nc.sync.dma_start(pos2_sb[:], pos2)
-        for lo, hi in ((0, T // 2), (T // 2, FUSED)):
-            nc.sync.dma_start(gates[:, lo:hi], gate[0, :, lo:hi])
+        nc.sync.dma_start(gates[:], gate[0, :, 0:FUSED])
 
         banks = []
 
@@ -268,12 +268,9 @@ def tile_moe_pln_lin_relu_kernel(
         store(0, QUARTER)
         multiply(1, T // 2, FUSED)
         multiply(0, FUSED, T)
-        add(nc.vector, QUARTER, FUSED)
-        store(QUARTER, FUSED)
-
-        halves = ((FUSED, T - P), (T - P, T))
-        for lo, hi in halves:
-            multiply(1, lo, hi)
-        for lo, hi in halves:
+        add(nc.vector, QUARTER, SPACER)
+        store(QUARTER, SPACER)
+        multiply(1, FUSED, T)
+        for lo, hi in ((SPACER, FUSED), (FUSED, T)):
             add(nc.vector, lo, hi)
-        store(FUSED, T)
+            store(lo, hi)

@@ -37,7 +37,7 @@ SPREAD = ((1, 0, T // 2), (1, T // 2, T), (0, FUSED, T))
 EXPERTS_A_LOAD = 2
 BURST = 256
 
-VECTOR_SHARES = (256, 160, 160)
+VECTOR_SHARES = (256, 160, 144)
 PASS1_LOADS = ((0, 256), (256, 512), (512, 768), (768, 896), (896, 1024))
 PASS1_QUANTISE = ((0, 512), (512, 768), (768, 896), (896, 1024))
 PASS1_GATHERS = ((0, 896), (896, 1536), (1536, 1920), (1920, 2048))
@@ -75,7 +75,8 @@ def tile_moe_pln_lin_relu_kernel(
 
         nc.vector.memset(warm[:], 0.0)
         nc.scalar.activation(warm[:, 0:1], warm[:, 1:2], RELU)
-        nc.vector.memset(x_scales[:].bitcast(I32), 0)
+        nc.vector.memset(x_scales[:, 0:T].bitcast(I32), 0)
+        nc.vector.memset(x_scales[:, T:].bitcast(I32), 0)
         nc.vector.memset(w_scales[:].bitcast(I32), 0)
         make_identity(nc, identity[:])
         nc.vector.memset(gate_rows[:], 0.0)
@@ -176,7 +177,8 @@ def tile_moe_pln_lin_relu_kernel(
         cast_pass0(T // 2, T - QUARTER, VECTOR_SHARES[1])
         cast_pass0(T - QUARTER, T, VECTOR_SHARES[2])
         quantize(0, T // 2, T - QUARTER)
-        quantize(0, T - QUARTER, T)
+        quantize(0, T - QUARTER, T - P)
+        quantize(0, T - P, T)
 
         gather_codes(slot_codes[0][:, 0:EARLY], 0, 0, EARLY, 2 * EARLY)
         for lo, hi in PASS1_LOADS:

@@ -75,12 +75,14 @@ def tile_moe_pln_lin_relu_kernel(
 
         nc.vector.memset(warm[:], 0.0)
         nc.scalar.activation(warm[:, 0:1], warm[:, 1:2], RELU)
-        nc.vector.memset(x_scales[:, 0:T].bitcast(I32), 0)
-        nc.vector.memset(x_scales[:, T:].bitcast(I32), 0)
-        nc.vector.memset(w_scales[:].bitcast(I32), 0)
+        for s in range(0, 2 * SLOTS, T // 2):
+            nc.vector.memset(x_scales[:, s : s + T // 2].bitcast(I32), 0)
+        for s in range(0, E * N, 2 * N):
+            nc.vector.memset(w_scales[:, s : s + 2 * N].bitcast(I32), 0)
         make_identity(nc, identity[:])
         nc.vector.memset(gate_rows[:], 0.0)
-        nc.vector.memset(words[:, 2 * T :].bitcast(I32), 0)
+        for s in range(2 * T, T + 2 * EARLY, 2 * P):
+            nc.vector.memset(words[:, s : s + 2 * P].bitcast(I32), 0)
 
         grouped = [keep.tile([P, T, PACK], BF16, name=f"grouped{a}", align_bytes=64) for a in range(PASSES)]
         raw = {}

from contextlib import ExitStack

import concourse.mybir as mybir
from concourse.masks import make_identity

K, T, E, C, N = 1024, 1024, 8, 256, 128
SLOTS = E * C
FLOPS = 2 * SLOTS * K * N

F32 = mybir.dt.float32
BF16 = mybir.dt.bfloat16
I32 = mybir.dt.int32
U32 = mybir.dt.uint32
U16 = mybir.dt.uint16
U8 = mybir.dt.uint8
FP8X4 = mybir.dt.float8_e4m3fn_x4
FP4X4 = mybir.dt.float4_e2m1fn_x4
COPY = mybir.ActivationFunctionType.Copy
RELU = mybir.ActivationFunctionType.Relu
MULT = mybir.AluOpType.mult
ADD = mybir.AluOpType.add
MAX = mybir.AluOpType.max

P = 128
K_PASS = 512
PASSES = K // K_PASS
PACK = 4
LIST_ROWS = 16
BANKS = 8
FIRST_ROW = (4, 0)
HALF = C // 2
EARLY = SLOTS - HALF
QUARTER = T // 4
FUSED = 3 * QUARTER
SPACER = FUSED - 192
SPREAD = ((1, 0, T // 2), (1, T // 2, T), (0, FUSED, T))
EXPERTS_A_LOAD = 2
BURST = 256

VECTOR_SHARES = (256, 160, 144)
PASS1_LOADS = ((0, 256), (256, 512), (512, 768), (768, 896), (896, 1024))
PASS1_QUANTISE = ((0, 512), (512, 768), (768, 896), (896, 1024))
PASS1_GATHERS = ((0, 896), (896, 1536), (1536, 1920), (1920, 2048))


def tile_moe_pln_lin_relu_kernel(
    tc, xT, w8_words, w8_scales, w4_words, w4_scales, b, gate, offs, pos1, pos2, out
):
    nc = tc.nc
    with ExitStack() as ctx:
        keep = ctx.enter_context(tc.tile_pool(name="keep", bufs=1))
        psum = ctx.enter_context(tc.psum_pool(name="psum", bufs=1))

        offs_sb = keep.tile([P, SLOTS // LIST_ROWS], U16, name="offs_sb", align_bytes=BURST)
        pos1_sb = keep.tile([P, T // LIST_ROWS], U16, name="pos1_sb")
        pos2_sb = keep.tile([P, T // LIST_ROWS], U16, name="pos2_sb")
        w8_sb = keep.tile([P, E, 4 * N], U8, name="w8_sb", align_bytes=BURST)
        w4_sb = keep.tile([P, E, 2 * N], U8, name="w4_sb", align_bytes=BURST)
        w_scales = keep.tile([P, E * N], U8, name="w_scales", align_bytes=64)
        x_scales = keep.tile([P, 2 * SLOTS], U8, name="x_scales", align_bytes=64)
        slot_scales = keep.tile([P, SLOTS], U8, name="slot_scales", align_bytes=64)
        words = keep.tile([P, T + 2 * EARLY], U32, name="words", align_bytes=64)
        x_codes = [words[:, T:], words[:, :]]
        slot_codes = [
            keep.tile([P, (EARLY, SLOTS)[a]], U32, name=f"slot_codes{a}", align_bytes=64) for a in range(PASSES)
        ]
        bias = keep.tile([P, E], F32, name="bias")
        gates = keep.tile([P, FUSED], F32, name="gates", align_bytes=BURST)
        gate_blocks = [(g, s) for g, first, last in SPREAD for s in range(first, last, P)]
        gate_rows = keep.tile([P, P], F32, name="gate_rows", align_bytes=BURST)
        gate_columns = keep.tile([P, len(gate_blocks)], F32, name="gate_columns")
        y = keep.tile([P, SLOTS], F32, name="y")
        warm = keep.tile([P, 8], F32, name="warm")
        identity = keep.tile([P, P], F32, name="identity")

        nc.vector.memset(warm[:], 0.0)
        nc.scalar.activation(warm[:, 0:1], warm[:, 1:2], RELU)
        for s in range(0, 2 * SLOTS, T // 2):
            nc.vector.memset(x_scales[:, s : s + T // 2].bitcast(I32), 0)
        for s in range(0, E * N, 2 * N):
            nc.vector.memset(w_scales[:, s : s + 2 * N].bitcast(I32), 0)
        make_identity(nc, identity[:])
        nc.vector.memset(gate_rows[:], 0.0)
        for s in range(2 * T, T + 2 * EARLY, 2 * P):
            nc.vector.memset(words[:, s : s + 2 * P].bitcast(I32), 0)

        grouped = [keep.tile([P, T, PACK], BF16, name=f"grouped{a}", align_bytes=64) for a in range(PASSES)]
        raw = {}

        def x_rows(a, lo, hi):
            return xT[K_PASS * a : K_PASS * (a + 1), lo:hi].rearrange("(p j) t -> p j t", j=PACK)

        second_half = keep.tile([P, PACK, T // 2], F32, name="whole", align_bytes=BURST)
        first_half = keep.tile([P, PACK, T // 2], F32, name="front", align_bytes=BURST)

        def load_pass0(j0, j1, lo, hi):
            tile, first = (first_half, 0) if lo < T // 2 else (second_half, T // 2)
            raw[0, lo] = tile[:, :, lo - first : hi - first]
            middle = (j0 + j1) // 2
            for queue, r0, r1 in ((nc.sync, j0, middle), (nc.scalar, middle, j1)):
                queue.dma_start(tile[:, r0:r1, lo - first : hi - first], x_rows(0, lo, hi)[:, r0:r1, :])

        def load_pass1(lo, hi):
            raw[1, lo] = keep.tile([P, PACK, hi - lo], F32, name=f"raw1_0_{lo}", align_bytes=BURST)
            nc.sync.dma_start(raw[1, lo][:], x_rows(1, lo, hi))

        def scalar_copy(dst, src):
            nc.scalar.activation(dst, src, COPY)

        def interleave(copy, a, first, lo, hi):
            copy(
                grouped[a][:, lo:hi, :].rearrange("p (c i) j -> p c j i", i=4),
                raw[a, first][:, :, lo - first : hi - first].rearrange("p j (c i) -> p c j i", i=4),
            )

        def cast_pass0(lo, hi, vector_tokens):
            interleave(nc.vector.tensor_copy, 0, lo, lo, lo + vector_tokens)
            interleave(scalar_copy, 0, lo, lo + vector_tokens, hi)

        def quantize(a, lo, hi):
            nc.vector.quantize_mx(
                out=x_codes[a][:, lo:hi].bitcast(FP8X4),
                scales=x_scales[FIRST_ROW[a] : P, lo:hi],
                in_=grouped[a][:, lo:hi, :].rearrange("p t j -> p (t j)"),
            )

        def entries(list_sb, lo, hi):
            return list_sb[:, lo // LIST_ROWS : hi // LIST_ROWS]

        def gather_codes(dst, a, lo, hi, window):
            nc.vector.tensor_copy(dst, x_codes[a][:, 0:window].indirect(entries(offs_sb, lo, hi)))

        load_pass0(0, 4, 0, T // 2)
        load_pass0(0, 2, T // 2, T)
        load_pass0(2, 4, T // 2, T - QUARTER)
        load_pass0(2, 4, T - QUARTER, T)
        nc.sync.dma_start(offs_sb[:], offs)
        for lo, hi in PASS1_LOADS:
            load_pass1(lo, hi)
        for e in range(0, E, EXPERTS_A_LOAD):
            experts = slice(e, e + EXPERTS_A_LOAD)
            nc.sync.dma_start(
                w8_sb[:, experts, :].bitcast(I32), w8_words[experts, 0].rearrange("e p n r -> p e (n r)").bitcast(I32)
            )
        for g, first in ((0, FUSED), (1, 0)):
            row = gate_blocks.index((g, first))
            nc.sync.dma_start(
                gate_rows[row : row + (T - first) // P, :], gate[g, 0, first:T].rearrange("(r s) -> r s", s=P)
            )
        for e in range(0, E, EXPERTS_A_LOAD):
            experts = slice(e, e + EXPERTS_A_LOAD)
            nc.sync.dma_start(
                w4_sb[:, experts, :].bitcast(I32), w4_words[experts, 0].rearrange("e p m -> p e m").bitcast(I32)
            )
        for source, first in ((w8_scales, FIRST_ROW[0]), (w4_scales, FIRST_ROW[1])):
            for q in range(4):
                nc.sync.dma_start(
                    w_scales[32 * q + first : 32 * q + first + 4, :].bitcast(I32).rearrange("q (e n) -> q e n", e=E),
                    source[:, 0, 4 * q : 4 * q + 4, :].rearrange("e q n -> q e n").bitcast(I32),
                )
        nc.sync.dma_start(bias[:], b)
        nc.sync.dma_start(pos1_sb[:], pos1)
        nc.sync.dma_start(pos2_sb[:], pos2)
        nc.sync.dma_start(gates[:], gate[0, :, 0:FUSED])

        banks = []

        def new_bank():
            banks.append(psum.tile([P, 2 * C], F32, name=f"acc{len(banks) % BANKS}"))
            return banks[-1]

        turned_rows = new_bank()
        nc.tensor.transpose(turned_rows[:, 0:P], gate_rows[:], identity[:])
        scalar_copy(gate_columns[:], turned_rows[:, 0 : len(gate_blocks)])

        cast_pass0(0, T // 2, VECTOR_SHARES[0])
        quantize(0, 0, QUARTER)
        quantize(0, QUARTER, T // 2)
        cast_pass0(T // 2, T - QUARTER, VECTOR_SHARES[1])
        cast_pass0(T - QUARTER, T, VECTOR_SHARES[2])
        quantize(0, T // 2, T - QUARTER)
        quantize(0, T - QUARTER, T - P)
        quantize(0, T - P, T)

        gather_codes(slot_codes[0][:, 0:EARLY], 0, 0, EARLY, 2 * EARLY)
        for lo, hi in PASS1_LOADS:
            interleave(scalar_copy, 1, lo, lo, hi)
        for lo, hi in PASS1_QUANTISE:
            quantize(1, lo, hi)

        late_codes = keep.tile([P, HALF], U32, name=f"raw1_0_{PASS1_LOADS[-1][0]}", align_bytes=BURST)
        gather_codes(late_codes[:], 0, EARLY, SLOTS, T)
        nc.vector.tensor_copy(slot_scales[:, 0:SLOTS], x_scales[:].indirect(entries(offs_sb, 0, SLOTS)))

        def one_pass(a, acc, lo, hi, stop):
            e = lo // C
            weights = w8_sb[:, e, :].bitcast(FP8X4) if a == 0 else w4_sb[:, e, :].bitcast(FP4X4)
            codes = late_codes[:] if (a, lo) == (0, EARLY) else slot_codes[a][:, lo:hi]
            nc.tensor.matmul_mx(
                out=acc,
                lhsT=weights,
                lhsT_scale=w_scales[FIRST_ROW[a] : P, e * N : (e + 1) * N],
                rhs=codes.bitcast(FP8X4),
                rhs_scale=slot_scales[FIRST_ROW[a] : P, lo:hi],
                start=(a == 0),
                stop=stop,
            )

        groups = [(s, s + C) for s in range(0, SLOTS - 2 * C, C)]
        groups = groups + [(s, s + HALF) for s in range(SLOTS - 2 * C, SLOTS, HALF)]
        sums = {}

        def open_group(lo, hi):
            sums[lo] = new_bank()
            one_pass(0, sums[lo][:, 0 : hi - lo], lo, hi, False)

        def close_group(lo, hi):
            for s in range(lo, hi, HALF):
                one_pass(1, sums[lo][:, s - lo : s - lo + HALF], s, s + HALF, s + HALF == hi)
            column = bias[:, lo // C : lo // C + 1]
            if hi == SLOTS - HALF:
                nc.vector.tensor_scalar(y[:, lo:hi], sums[lo][:, 0 : hi - lo], column, 0.0, ADD, MAX)
            else:
                nc.scalar.activation(y[:, lo:hi], sums[lo][:, 0 : hi - lo], RELU, bias=column)

        for lo, hi in groups[:BANKS]:
            open_group(lo, hi)
        for first, last in PASS1_GATHERS:
            gather_codes(slot_codes[1][:, first:last], 1, first, last, 2 * T if first == 0 else T)
            for lo, hi in groups:
                if first < hi <= last:
                    close_group(lo, hi)
            if first == 0:
                for lo, hi in groups[BANKS:]:
                    open_group(lo, hi)

        fetched = keep.tile([P, 2, T], F32, name="fetched")
        products = keep.tile([P, 2, T], F32, name="products")
        result = keep.tile([P, T], F32, name="result", align_bytes=BURST)
        pos_sb = (pos1_sb, pos2_sb)

        spread = {}
        for g, first, last in SPREAD:
            bank = new_bank()
            for s in range(first, last, P):
                r = gate_blocks.index((g, s))
                nc.tensor.transpose(
                    bank[:, s - first : s - first + P], gate_columns[:, r : r + 1].to_broadcast([P, P]), identity[:]
                )
                spread[g, s] = (bank, first)

        def looked_up(g, lo, hi):
            return y[:].indirect(entries(pos_sb[g], lo, hi))

        def multiply(g, lo, hi):
            bank, first = spread[g, lo]
            nc.vector.tensor_tensor(products[:, g, lo:hi], fetched[:, g, lo:hi], bank[:, lo - first : hi - first], MULT)

        def add(engine, lo, hi):
            engine.tensor_tensor(result[:, lo:hi], products[:, 0, lo:hi], products[:, 1, lo:hi], ADD)

        def store(lo, hi):
            nc.sync.dma_start(out[:, lo:hi], result[:, lo:hi])

        for g, lo, hi in ((1, 0, T // 2), (1, T // 2, FUSED), (0, FUSED, T), (1, FUSED, T)):
            scalar_copy(fetched[:, g, lo:hi], looked_up(g, lo, hi))
        nc.vector.tensor_tensor(products[:, 0, 0:FUSED], looked_up(0, 0, FUSED), gates[:], MULT)

        multiply(1, 0, QUARTER)
        multiply(1, QUARTER, T // 2)
        add(nc.gpsimd, 0, QUARTER)
        store(0, QUARTER)
        multiply(1, T // 2, FUSED)
        multiply(0, FUSED, T)
        add(nc.vector, QUARTER, SPACER)
        store(QUARTER, SPACER)
        multiply(1, FUSED, T)
        for lo, hi in ((SPACER, FUSED), (FUSED, T)):
            add(nc.vector, lo, hi)
            store(lo, hi)
